import numpy as np
import ml_dtypes


def mxq(x, axis, fmt="e4m3"):
    dtype, down = {"e4m3": (ml_dtypes.float8_e4m3fn, 7), "e5m2": (ml_dtypes.float8_e5m2, 14)}[fmt]
    v = np.moveaxis(np.asarray(x, np.float32).astype(ml_dtypes.bfloat16).astype(np.float64), axis, -1)
    blocks = v.reshape(v.shape[:-1] + (-1, 32))
    amax = np.abs(blocks).max(-1, keepdims=True)
    byte = np.maximum(np.where(amax > 0, np.frexp(amax)[1] - 1 + 127, 0) - down, 1)
    scale = np.exp2(byte - 127.0)
    codes = (blocks / scale).astype(np.float32).astype(dtype).astype(np.float64)
    return np.moveaxis((codes * scale).reshape(v.shape), -1, axis)


WIDE = False


def mx_kscale(k):
    if not WIDE:
        return np.ones(k)
    levels = np.array([10, -10, 5, -5, 0])
    if k % 512:
        return np.exp2(np.random.permutation(np.resize(levels, k // 32))).repeat(32)
    a = np.empty((k // 512, 16))
    for p in range(k // 512):
        a[p, :8] = np.random.permutation(np.resize(levels, 8))
        for g in range(8):
            far = levels[np.abs(levels - a[p, g]) >= 10]
            a[p, g + 8] = far[np.random.randint(len(far))]
    return np.exp2(a.ravel()).repeat(32)


def f64(x):
    return np.asarray(x).astype(np.float64)


def striped(idx):
    return np.tile(np.asarray(idx).reshape(-1, 16).T, (8, 1)).astype(np.uint16)


def unstriped(offs):
    return offs[:16].T.reshape(-1).astype(np.int64)


E2M1 = np.array([0.0, 0.5, 1.0, 1.5, 2.0, 3.0, 4.0, 6.0, -0.0, -0.5, -1.0, -1.5, -2.0, -3.0, -4.0, -6.0])


def pack_weight(w, fmt):
    k, n = w.shape
    w = f64(np.asarray(w, np.float32).astype(ml_dtypes.bfloat16)).reshape(k // 32, 32, n)
    amax = np.abs(w).max(1)
    if fmt == "e4m3":
        byte = np.frexp(amax)[1] - 1 + 127 - 7
    else:
        mant, ex = np.frexp(amax / 6.0)
        byte = np.where(mant > 0.5, ex, ex - 1) + 127
    byte = np.clip(np.where(amax > 0, byte, 1), 1, 254)
    scaled = (w * np.exp2(127.0 - byte)[:, None, :]).reshape(k, n).astype(np.float32)
    by_word = np.ascontiguousarray(scaled.reshape(k // 512, 128, 4, n).transpose(0, 1, 3, 2))
    if fmt == "e4m3":
        words = by_word.astype(ml_dtypes.float8_e4m3fn).view(np.uint8)
    else:
        c = by_word.astype(ml_dtypes.float4_e2m1fn).view(np.uint8) & 0xF
        words = (c[..., 0::2] | (c[..., 1::2] << 4)).reshape(k // 512, 128, 2 * n)
    return np.ascontiguousarray(words), np.ascontiguousarray(byte.astype(np.uint8).reshape(k // 512, 16, n))


def unpack_weight(words, scales, fmt):
    g, _, n = scales.shape
    words = np.ascontiguousarray(words).reshape(g, 128, n, -1)
    if fmt == "e4m3":
        vals = words.view(ml_dtypes.float8_e4m3fn).astype(np.float64)
    else:
        nib = np.empty((g, 128, n, 4), np.uint8)
        nib[..., 0::2] = words & 0xF
        nib[..., 1::2] = words >> 4
        vals = E2M1[nib]
    vals = vals * np.repeat(np.exp2(scales.astype(np.float64) - 127.0), 8, axis=1)[..., None]
    return vals.transpose(0, 1, 3, 2).reshape(g * 512, n)


def softplus(v):
    return np.log(1.0 + np.exp(v))


def sigmoid(v):
    return 1.0 / (1.0 + np.exp(-v))


D, E, T, I, Q = 512, 512, 2048, 512, 128


def setup_inputs():
    n = np.random.standard_normal
    idx = np.random.permutation(T)[:I]
    fd = mx_kscale(D)
    fe = mx_kscale(E)
    keysp = pack_weight(n((D, T)) / fd[:, None], "e4m3")
    valsp = pack_weight(n((E, T)) / fe[:, None], "e4m3")
    return {
        "query": (n((D, Q)) * 1.0 / np.sqrt(D) * fd[:, None]).astype(np.float32),
        "keys_words": keysp[0],
        "keys_scales": keysp[1],
        "ceil_t": np.tile(np.random.uniform(1.0, 4.0, T), (128, 1)).astype(np.float32),
        "halfp": np.tile(np.random.uniform(0.4, 1.5, T), (128, 1)).astype(np.float32),
        "sharp": (np.random.uniform(1.5, 3.0, (Q, 1))).astype(np.float32),
        "share": (np.random.uniform(0.5, 0.9, (Q, 1))).astype(np.float32),
        "gout": (n((E, Q)) * 1 / np.sqrt(E) * fe[:, None]).astype(np.float32),
        "vals_words": valsp[0],
        "vals_scales": valsp[1],
        "dquery": (n((D, Q)) * 1.0 / np.sqrt(D) * fd[:, None]).astype(np.float32),
        "base": (0.5 * n((Q, T))).astype(np.float32),
        "offs": striped(idx),
    }


def reference(query, keys_words, keys_scales, ceil_t, halfp, sharp, share, gout, vals_words, vals_scales, dquery, base, offs):
    idx = unstriped(offs)
    keysu = unpack_weight(keys_words, keys_scales, "e4m3")
    valsu = unpack_weight(vals_words, vals_scales, "e4m3")
    queryq = mxq(f64(query), 0, "e4m3")
    keysidxg = keysu[:, idx]
    a = queryq.T @ keysidxg
    dqueryq = mxq(f64(dquery), 0, "e4m3")
    ta = dqueryq.T @ keysidxg
    fa = softplus(a * 2.0)
    s = fa * f64(ceil_t)[:1][:, idx] / (fa + f64(halfp)[:1][:, idx])
    p = np.exp(s - np.max(s, axis=1, keepdims=True))
    s2 = s * f64(sharp)
    p2 = np.exp(s2 - np.max(s2, axis=1, keepdims=True))
    goutq = mxq(f64(gout), 0, "e4m3")
    valsidxg = valsu[:, idx]
    c0 = goutq.T @ valsidxg
    dr2 = c0 * (-1.0) * (1.0 - f64(share))
    dp2 = dr2 / np.sum(p2, axis=1, keepdims=True) + np.sum(dr2 * p2 / np.square(np.sum(p2, axis=1, keepdims=True)) * (-1.0), axis=1, keepdims=True)
    ds2 = dp2 * p2
    dr = c0 * f64(share)
    dp = dr / np.sum(p, axis=1, keepdims=True) + np.sum(dr * p / np.square(np.sum(p, axis=1, keepdims=True)) * (-1.0), axis=1, keepdims=True)
    ds = ds2 * f64(sharp) + dp * p
    dfa = ds / (fa + f64(halfp)[:1][:, idx]) * f64(ceil_t)[:1][:, idx] - ds * fa * f64(ceil_t)[:1][:, idx] / np.square(fa + f64(halfp)[:1][:, idx])
    tfa = ta * 2.0 * sigmoid(a * 2.0)
    ts = (tfa * f64(ceil_t)[:1][:, idx] - tfa * fa * f64(ceil_t)[:1][:, idx] / (fa + f64(halfp)[:1][:, idx])) / (fa + f64(halfp)[:1][:, idx])
    tp = ts * p
    ts2 = ts * f64(sharp)
    tp2 = ts2 * p2
    tdp2 = np.sum(tp2, axis=1, keepdims=True) * dr2 / np.square(np.sum(p2, axis=1, keepdims=True)) * (-1.0) + np.sum((tp2 * dr2 - np.sum(tp2, axis=1, keepdims=True) * np.sum(p2, axis=1, keepdims=True) * 2.0 * dr2 * p2 / np.square(np.sum(p2, axis=1, keepdims=True))) / np.square(np.sum(p2, axis=1, keepdims=True)) * (-1.0), axis=1, keepdims=True)
    tds2 = tdp2 * p2 + tp2 * dp2
    tdp = np.sum(tp, axis=1, keepdims=True) * dr / np.square(np.sum(p, axis=1, keepdims=True)) * (-1.0) + np.sum((tp * dr - np.sum(tp, axis=1, keepdims=True) * np.sum(p, axis=1, keepdims=True) * 2.0 * dr * p / np.square(np.sum(p, axis=1, keepdims=True))) / np.square(np.sum(p, axis=1, keepdims=True)) * (-1.0), axis=1, keepdims=True)
    tds = tds2 * f64(sharp) + tdp * p + tp * dp
    tdfa = (tds - tfa * ds / (fa + f64(halfp)[:1][:, idx])) / (fa + f64(halfp)[:1][:, idx]) * f64(ceil_t)[:1][:, idx] - (tds * fa * f64(ceil_t)[:1][:, idx] + tfa * f64(ceil_t)[:1][:, idx] * ds - tfa * (fa + f64(halfp)[:1][:, idx]) * 2.0 * ds * fa * f64(ceil_t)[:1][:, idx] / np.square(fa + f64(halfp)[:1][:, idx])) / np.square(fa + f64(halfp)[:1][:, idx])
    tda = (tdfa * sigmoid(a * 2.0) + ta * 2.0 * sigmoid(a * 2.0) * (1.0 - sigmoid(a * 2.0)) * dfa) * 2.0
    gs = tda * 512.0
    gf = np.zeros((Q, T))
    gf[:, idx] = gs
    y = f64(base) + gf
    return y

@@ -1,0 +1,277 @@
+from contextlib import ExitStack
+
+import concourse.mybir as mybir
+from concourse.masks import make_identity
+
+D, T, I, Q = 512, 2048, 512, 128
+FLOPS = 3 * 2 * D * I * Q
+
+F32 = mybir.dt.float32
+BF16 = mybir.dt.bfloat16
+I32 = mybir.dt.int32
+U32 = mybir.dt.uint32
+U16 = mybir.dt.uint16
+U8 = mybir.dt.uint8
+FP8X4 = mybir.dt.float8_e4m3fn_x4
+ALU = mybir.AluOpType
+ACT = mybir.ActivationFunctionType
+P = 128
+BLOCKS = I // P
+HALF = I // 2
+CHUNK = 512
+
+
+def tile_attend_hvsaturating_twoheats_s_kernel(
+    tc, query, keys_words, keys_scales, ceil_t, halfp, sharp, share, gout, vals_words, vals_scales, dquery, base, offs, out
+):
+    nc = tc.nc
+    vec, act, pe, pool_eng = nc.vector, nc.scalar, nc.tensor, nc.gpsimd
+    with ExitStack() as ctx:
+        sb = ctx.enter_context(tc.tile_pool(name="sb", bufs=1))
+        ps = ctx.enter_context(tc.psum_pool(name="ps", bufs=1))
+
+        def wide(name):
+            return sb.tile([P, I], F32, name=name)
+
+        def load_scales(name, scales, zeroer):
+            tile = sb.tile([P, T + 4], U8, name=name, tag=name)
+            zeroer.memset(tile[:].bitcast(I32), 0)
+            for quad in range(4):
+                nc.sync.dma_start(out=tile[32 * quad : 32 * quad + 4, 0:T].bitcast(I32), in_=scales[0, 4 * quad : 4 * quad + 4, :].bitcast(I32))
+            return tile
+
+        def load_words(name, words, tag):
+            tile = sb.tile([P, T], U32, name=name, tag=tag)
+            nc.sync.dma_start(out=tile[:].bitcast(I32), in_=words[0].rearrange("p n t -> p (n t)").bitcast(I32))
+            return tile
+
+        def load_row(name, table, tag, zeroer):
+            tile = sb.tile([P, T + 1], F32, name=name, tag=tag)
+            zeroer.memset(tile[:], 0.0)
+            nc.sync.dma_start(out=tile[0:1, 0:T], in_=table[0:1, :])
+            return tile
+
+        def load_rows(name, rows, tag):
+            raw = sb.tile([P, 4, Q], F32, name=name, tag=tag)
+            nc.sync.dma_start(out=raw[:], in_=rows.rearrange("(p j) w -> p j w", j=4))
+            return raw
+
+        def quantise(name, raw, cast):
+            grouped = sb.tile([P, Q, 4], BF16, name=name + "_bf", align_bytes=64)
+            cast(out=grouped[:], in_=raw[:].rearrange("p j w -> p w j"))
+            codes = sb.tile([P, Q], U32, name=name + "_codes", align_bytes=64)
+            scales = sb.tile([P, Q], U8, name=name + "_scales", align_bytes=64)
+            vec.quantize_mx(out=codes[:].bitcast(FP8X4), scales=scales[:], in_=grouped[:].rearrange("p w j -> p (w j)"))
+            return codes, scales
+
+        def gather(name, window, dtype):
+            picked = sb.tile([P, I], dtype, name=name, align_bytes=64)
+            vec.tensor_copy(out=picked[:], in_=window[:, 0:T].indirect(offsets[:]))
+            return picked
+
+        def product(name, rows, words, scales):
+            bank = ps.tile([P, I], F32, name=name)
+            pe.matmul_mx(out=bank[:], lhsT=rows[0][:].bitcast(FP8X4), lhsT_scale=rows[1][:], rhs=words[:].bitcast(FP8X4), rhs_scale=scales[:], start=True, stop=True)
+            return bank
+
+        def turn(name, picked, tag):
+            bank = ps.tile([P, BLOCKS, P], F32, name=name + "_turned", tag=tag)
+            for b in range(BLOCKS):
+                pe.transpose(bank[:, b, :], picked[:, b * P : (b + 1) * P], ident[:])
+            return bank
+
+        def scores_by_slot(name, rows, words, scales):
+            bank = ps.tile([P, BLOCKS, Q], F32, name=name)
+            for b in range(BLOCKS):
+                cs = slice(b * P, (b + 1) * P)
+                pe.matmul_mx(out=bank[:, b, :], lhsT=words[:, cs].bitcast(FP8X4), lhsT_scale=scales[:, cs], rhs=rows[0][:].bitcast(FP8X4), rhs_scale=rows[1][:], start=True, stop=True)
+            return bank[:].rearrange("p b q -> p (b q)")
+
+        def turn_into(bank, blocks, first, last):
+            for b in range(BLOCKS):
+                pe.matmul(out=bank[:, b * P : (b + 1) * P], lhsT=blocks[b], rhs=ident[:], is_transpose=True, start=first and b == 0, stop=last and b == BLOCKS - 1)
+
+        def blocks_of(tile):
+            return [tile[:, b * P : (b + 1) * P] for b in range(BLOCKS)]
+
+        offsets = sb.tile([P, I // 16], U16, name="offsets")
+        nc.sync.dma_start(offsets[:], offs)
+        q_raw = load_rows("q_raw", query, "rows_a")
+        k_words = load_words("k_words", keys_words, "win_k")
+        k_scales = load_scales("k_scales", keys_scales, vec)
+        half_win = load_row("half_win", halfp, "win_h", pool_eng)
+        ceil_win = load_row("ceil_win", ceil_t, "win_c", vec)
+        ident = sb.tile([P, P], F32, name="ident")
+        make_identity(nc, ident[:])
+        v_scales = load_scales("v_scales", vals_scales, pool_eng)
+        sharp_c = sb.tile([P, 1], F32, name="sharp_c")
+        pool_eng.dma_start(out=sharp_c[:], in_=sharp)
+        share_c = sb.tile([P, 1], F32, name="share_c")
+        pool_eng.dma_start(out=share_c[:], in_=share)
+
+        k_bytes = gather("k_bytes", k_scales, U8)
+        q_mx = quantise("q", q_raw, act.copy)
+        dq_raw = load_rows("dq_raw", dquery, "rows_a")
+        k_codes = gather("k_codes", k_words, U32)
+        a = scores_by_slot("a", q_mx, k_codes, k_bytes)
+
+        half_row = wide("half_row")
+        act.activation(out=half_row[:], in_=half_win[:].indirect(offsets[:]), func=ACT.Copy)
+        half_turned = turn("half", half_row, "bank_g")
+        ceil_turned = turn("ceil", gather("ceil_row", ceil_win, F32), "bank_t")
+        v_words = load_words("v_words", vals_words, "win_h")
+        base_sb = sb.tile([P, T], F32, name="base_sb", tag="k_scales")
+        nc.sync.dma_start(out=base_sb[:], in_=base)
+        placed = sb.tile([P, T], F32, name="placed", tag="win_k")
+        pool_eng.memset(placed[:], 0.0)
+
+        nth = wide("nth")
+        act.activation(out=nth[:], in_=a, func=ACT.Tanh, scale=-1.0)
+        th_abs = wide("th_abs")
+        vec.scalar_tensor_tensor(out=th_abs[:], in0=nth[:], scalar=-1.0, in1=nth[:], op0=ALU.mult, op1=ALU.max)
+        lg = wide("lg")
+        act.activation(out=lg[:], in_=th_abs[:], func=ACT.Ln, scale=0.5, bias=0.5)
+        rl = wide("rl")
+        vec.tensor_scalar(out=rl[:], in0=a, scalar1=0.0, scalar2=None, op0=ALU.max)
+
+        hh = sb.tile([P, BLOCKS], F32, name="hh")
+        cc = sb.tile([P, BLOCKS], F32, name="cc")
+        nk = sb.tile([P, BLOCKS], F32, name="nk")
+        c3 = sb.tile([P, BLOCKS], F32, name="c3")
+        vec.tensor_scalar(out=hh[:], in0=half_turned[:, :, 0], scalar1=0.5, scalar2=None, op0=ALU.mult)
+        vec.tensor_copy(out=cc[:], in_=ceil_turned[:, :, 0])
+        vec.scalar_tensor_tensor(out=nk[:], in0=cc[:], scalar=-1.0, in1=hh[:], op0=ALU.mult, op1=ALU.mult)
+        vec.scalar_tensor_tensor(out=c3[:], in0=nk[:], scalar=0.5, in1=hh[:], op0=ALU.mult, op1=ALU.add)
+        nkh = sb.tile([P, BLOCKS], F32, name="nkh")
+        vec.scalar_tensor_tensor(out=nkh[:], in0=cc[:], scalar=-0.5, in1=hh[:], op0=ALU.mult, op1=ALU.mult)
+
+        fh = wide("fh")
+        vec.scalar_tensor_tensor(out=fh[:], in0=lg[:], scalar=-0.5, in1=rl[:], op0=ALU.mult, op1=ALU.add)
+        y2 = wide("y2")
+        for b in range(BLOCKS):
+            act.activation(out=blocks_of(y2)[b], in_=blocks_of(fh)[b], func=ACT.Square, bias=hh[:, b : b + 1])
+        ly = wide("ly")
+        act.activation(out=ly[:], in_=y2[:], func=ACT.Ln)
+        qq = wide("qq")
+        act.activation(out=qq[:], in_=ly[:], func=ACT.Exp, scale=-1.0)
+
+        s_bank = ps.tile([P, I], F32, name="s_bank")
+        turn_into(s_bank, [cc[:, b : b + 1].to_broadcast([P, P]) for b in range(BLOCKS)], True, False)
+        nyk = wide("nyk")
+        for b in range(BLOCKS):
+            vec.tensor_scalar(out=blocks_of(nyk)[b], in0=blocks_of(fh)[b], scalar1=hh[:, b : b + 1], scalar2=nk[:, b : b + 1], op0=ALU.add, op1=ALU.mult)
+        dq_mx = quantise("dq", dq_raw, vec.tensor_copy)
+        ta = scores_by_slot("ta", dq_mx, k_codes, k_bytes)
+        pb1 = wide("pb1")
+        vec.scalar_tensor_tensor(out=pb1[:], in0=nth[:], scalar=1.0, in1=ta, op0=ALU.add, op1=ALU.mult)
+        f_bank = ps.tile([P, I], F32, name="f_bank")
+        turn_into(f_bank, blocks_of(pb1), True, False)
+        go_raw = load_rows("go_raw", gout, "rows_a")
+        go_mx = quantise("go", go_raw, vec.tensor_copy)
+        v_bytes = gather("v_bytes", v_scales, U8)
+        v_codes = gather("v_codes", v_words, U32)
+        c0 = product("c0", go_mx, v_codes, v_bytes)
+
+        cf = sb.tile([P, 3, 2], F32, name="cf")
+        shm1 = sb.tile([P, 1], F32, name="shm1")
+        sh256 = sb.tile([P, 1], F32, name="sh256")
+        pool_eng.tensor_scalar(out=shm1[:], in0=sharp_c[:], scalar1=-1.0, scalar2=1.0, op0=ALU.add, op1=ALU.mult)
+        pool_eng.tensor_scalar(out=sh256[:], in0=share_c[:], scalar1=-1.0, scalar2=256.0, op0=ALU.add, op1=ALU.mult)
+        nsharp = sb.tile([P, 1], F32, name="nsharp")
+        pool_eng.tensor_scalar(out=nsharp[:], in0=sharp_c[:], scalar1=-1.0, scalar2=0.0, op0=ALU.mult, op1=ALU.add)
+        for j in range(3):
+            pool_eng.tensor_scalar(out=cf[:, j, 0:1], in0=share_c[:], scalar1=256.0, scalar2=0.0, op0=ALU.mult, op1=ALU.add)
+        pool_eng.tensor_tensor(out=cf[:, 0, 1:2], in0=sh256[:], in1=sharp_c[:], op=ALU.mult)
+        pool_eng.tensor_tensor(out=cf[:, 1, 1:2], in0=cf[:, 0, 1:2], in1=sharp_c[:], op=ALU.mult)
+
+        pool_eng.tensor_tensor(out=cf[:, 2, 1:2], in0=cf[:, 0, 1:2], in1=shm1[:], op=ALU.mult)
+
+        nv = wide("nv")
+        vec.tensor_tensor(out=nv[:], in0=nyk[:], in1=qq[:], op=ALU.mult)
+        turn_into(s_bank, blocks_of(nv), False, True)
+        gq = wide("gq")
+        vec.scalar_tensor_tensor(out=gq[:], in0=nth[:], scalar=-1.0, in1=qq[:], op0=ALU.add, op1=ALU.mult)
+        tq = wide("tq")
+        vec.tensor_tensor(out=tq[:], in0=ta, in1=gq[:], op=ALU.mult)
+        tst = wide("tst")
+        for b in range(BLOCKS):
+            act.activation(out=blocks_of(tst)[b], in_=blocks_of(tq)[b], func=ACT.Copy, scale=nkh[:, b : b + 1])
+        low = sb.tile([P, 2], F32, name="low")
+        vec.tensor_reduce(out=low[:, 0:1], in_=s_bank[:], axis=mybir.AxisListType.X, op=ALU.max, negate=True)
+        ns2 = wide("ns2")
+        vec.tensor_scalar(out=ns2[:], in0=s_bank[:], scalar1=nsharp[:], scalar2=None, op0=ALU.mult, op1=ALU.min, accum_out=low[:, 1:2])
+        z = sb.tile([P, 2], F32, name="z")
+        p = [wide("p1"), wide("p2")]
+        act.activation(out=p[0][:], in_=s_bank[:], func=ACT.Exp, bias=low[:, 0:1], accum_out=z[:, 0:1])
+        act.activation(out=p[1][:], in_=ns2[:], func=ACT.Exp, scale=-1.0, bias=low[:, 1:2], accum_out=z[:, 1:2])
+
+        ts = ps.tile([P, I], F32, name="ts", tag="bank_t")
+        turn_into(ts, blocks_of(tst), True, True)
+        dqq = wide("dqq")
+        for b in range(BLOCKS):
+            vec.scalar_tensor_tensor(out=blocks_of(dqq)[b], in0=blocks_of(fh)[b], scalar=c3[:, b : b + 1], in1=blocks_of(tq)[b], op0=ALU.add, op1=ALU.mult)
+        turn_into(f_bank, blocks_of(dqq), False, True)
+        g4t = wide("g4t")
+        for b in range(BLOCKS):
+            act.activation(out=blocks_of(g4t)[b], in_=blocks_of(gq)[b], func=ACT.Copy, scale=nk[:, b : b + 1])
+        g_bank = ps.tile([P, I], F32, name="g_bank", tag="bank_g")
+        turn_into(g_bank, blocks_of(g4t), True, True)
+        rz = sb.tile([P, 2], F32, name="rz")
+        vec.reciprocal(out=rz[:], in_=z[:])
+        aa = sb.tile([P, 3, 2], F32, name="aa")
+        vec.tensor_tensor(out=aa[:], in0=cf[:], in1=rz[:].unsqueeze(1).to_broadcast([P, 3, 2]), op=ALU.mult)
+        c1 = sb.tile([P, 2], F32, name="c1")
+        vec.scalar_tensor_tensor(out=c1[:], in0=aa[:, 1, :], scalar=-1.0, in1=rz[:], op0=ALU.mult, op1=ALU.mult)
+
+        tb = sb.tile([P, 2], F32, name="tb")
+        m = sb.tile([P, 2], F32, name="m")
+        nn = sb.tile([P, 2], F32, name="nn")
+        ak = sb.tile([P, 2], F32, name="ak")
+        f = [wide("ff1"), wide("ff2")]
+        rc = [wide("rc1"), wide("rc2")]
+        for h in (1, 0):
+            col = slice(h, h + 1)
+            junk = wide("junk_t%d" % h)
+            vec.scalar_tensor_tensor(out=junk[:], in0=p[h][:], scalar=c1[:, col], in1=ts[:], op0=ALU.mult, op1=ALU.mult, accum_out=tb[:, col])
+        f2a = wide("f2a")
+        act.activation(out=f2a[:], in_=ts[:], func=ACT.Identity, scale=aa[:, 2, 1:2], bias=tb[:, 1:2])
+        act.activation(out=f[0][:], in_=f_bank[:], func=ACT.Identity, scale=aa[:, 0, 0:1], bias=tb[:, 0:1])
+        g4 = wide("g4")
+        act.copy(out=g4[:], in_=g_bank[:])
+        for h in range(2):
+            col = slice(h, h + 1)
+            vec.scalar_tensor_tensor(out=rc[h][:], in0=p[h][:], scalar=rz[:, col], in1=c0[:], op0=ALU.mult, op1=ALU.mult, accum_out=m[:, col])
+        for h in range(2):
+            col = slice(h, h + 1)
+            junk = wide("junk_n%d" % h)
+            vec.scalar_tensor_tensor(out=junk[:], in0=rc[h][:], scalar=aa[:, 1, col], in1=ts[:], op0=ALU.mult, op1=ALU.mult, accum_out=nn[:, col])
+            act.activation(out=ak[:, col], in_=tb[:, col], func=ACT.Identity, scale=m[:, col], bias=nn[:, col])
+
+        vec.scalar_tensor_tensor(out=f[1][:], in0=f_bank[:], scalar=aa[:, 0, 1:2], in1=f2a[:], op0=ALU.mult, op1=ALU.add)
+
+        probe = sb.tile([P, 4], F32, name="probe")
+        pool_eng.tensor_copy(out=probe[:, 0:1], in_=qq[:, 0:1])
+        pool_eng.tensor_copy(out=probe[:, 1:2], in_=tb[:, 0:1])
+        for part in range(2):
+            cs = slice(part * HALF, (part + 1) * HALF)
+            picks = offsets[:, part * (HALF // 16) : (part + 1) * (HALF // 16)]
+            b = [sb.tile([P, HALF], F32, name="b%d_%d" % (part, h)) for h in range(2)]
+            o = [sb.tile([P, HALF], F32, name="o%d_%d" % (part, h)) for h in range(2)]
+            for h in range(2):
+                vec.scalar_tensor_tensor(out=b[h][:], in0=c0[:, cs], scalar=m[:, h : h + 1], in1=f[h][:, cs], op0=ALU.subtract, op1=ALU.mult)
+            for h in range(2):
+                vec.scalar_tensor_tensor(out=o[h][:], in0=b[h][:], scalar=ak[:, h : h + 1], in1=p[h][:, cs], op0=ALU.subtract, op1=ALU.mult)
+            both = sb.tile([P, HALF], F32, name="both%d" % part)
+            vec.tensor_tensor(out=both[:], in0=o[0][:], in1=o[1][:], op=ALU.add)
+            if part == 0:
+                gs = sb.tile([P, HALF], F32, name="gs")
+                vec.tensor_tensor(out=gs[:], in0=both[:], in1=g4[:, cs], op=ALU.mult)
+                act.activation(out=placed[:].indirect(picks), in_=gs[:], func=ACT.Copy)
+            else:
+                vec.tensor_tensor(out=placed[:].indirect(picks), in0=both[:], in1=g4[:, cs], op=ALU.mult)
+
+        for c in range(T // CHUNK):
+            cs = slice(c * CHUNK, (c + 1) * CHUNK)
+            res = sb.tile([P, CHUNK], F32, name="res%d" % c)
+            vec.tensor_tensor(out=res[:], in0=placed[:, cs], in1=base_sb[:, cs], op=ALU.add)
+            nc.sync.dma_start(out=out[:, cs], in_=res[:])

@@ -30,23 +30,23 @@ def tile_attend_hvsaturating_twoheats_s_kernel(
         sb = ctx.enter_context(tc.tile_pool(name="sb", bufs=1))
         ps = ctx.enter_context(tc.psum_pool(name="ps", bufs=1))
 
-        def wide(name):
-            return sb.tile([P, I], F32, name=name)
+        def wide(name, tag=None):
+            return sb.tile([P, I], F32, name=name, tag=tag or name, align_bytes=64)
 
-        def load_scales(name, scales, zeroer):
-            tile = sb.tile([P, T + 4], U8, name=name, tag=name)
-            zeroer.memset(tile[:].bitcast(I32), 0)
+        def load_scales(name, scales, queue):
+            tile = sb.tile([P, T], U8, name=name, tag=name, align_bytes=64)
+            pool_eng.memset(tile[:].bitcast(I32), 0)
             for quad in range(4):
-                nc.sync.dma_start(out=tile[32 * quad : 32 * quad + 4, 0:T].bitcast(I32), in_=scales[0, 4 * quad : 4 * quad + 4, :].bitcast(I32))
+                queue.dma_start(out=tile[32 * quad : 32 * quad + 4, 0:T].bitcast(I32), in_=scales[0, 4 * quad : 4 * quad + 4, :].bitcast(I32))
             return tile
 
         def load_words(name, words, tag):
-            tile = sb.tile([P, T], U32, name=name, tag=tag)
+            tile = sb.tile([P, T], U32, name=name, tag=tag, align_bytes=64)
             nc.sync.dma_start(out=tile[:].bitcast(I32), in_=words[0].rearrange("p n t -> p (n t)").bitcast(I32))
             return tile
 
         def load_row(name, table, tag, zeroer):
-            tile = sb.tile([P, T + 1], F32, name=name, tag=tag)
+            tile = sb.tile([P, T + 1], F32, name=name, tag=tag, align_bytes=64)
             zeroer.memset(tile[:], 0.0)
             nc.sync.dma_start(out=tile[0:1, 0:T], in_=table[0:1, :])
             return tile
@@ -64,9 +64,11 @@ def tile_attend_hvsaturating_twoheats_s_kernel(
             vec.quantize_mx(out=codes[:].bitcast(FP8X4), scales=scales[:], in_=grouped[:].rearrange("p w j -> p (w j)"))
             return codes, scales
 
-        def gather(name, window, dtype):
-            picked = sb.tile([P, I], dtype, name=name, align_bytes=64)
-            vec.tensor_copy(out=picked[:], in_=window[:, 0:T].indirect(offsets[:]))
+        def gather(name, window, dtype, tag, parts=1):
+            picked = sb.tile([P, I], dtype, name=name, tag=tag, align_bytes=64)
+            n = I // parts
+            for j in range(parts):
+                vec.tensor_copy(out=picked[:, j * n : (j + 1) * n], in_=window[:, 0:T].indirect(offsets[:, j * n // 16 : (j + 1) * n // 16]))
             return picked
 
         def product(name, rows, words, scales):
@@ -80,10 +82,10 @@ def tile_attend_hvsaturating_twoheats_s_kernel(
                 pe.transpose(bank[:, b, :], picked[:, b * P : (b + 1) * P], ident[:])
             return bank
 
-        def scores_by_slot(name, rows, words, scales):
-            bank = ps.tile([P, BLOCKS, Q], F32, name=name)
-            for b in range(BLOCKS):
-                cs = slice(b * P, (b + 1) * P)
+        def scores_by_slot(name, rows, words, scales, first, count):
+            bank = ps.tile([P, count, Q], F32, name=name)
+            for b in range(count):
+                cs = slice((first + b) * P, (first + b + 1) * P)
                 pe.matmul_mx(out=bank[:, b, :], lhsT=words[:, cs].bitcast(FP8X4), lhsT_scale=scales[:, cs], rhs=rows[0][:].bitcast(FP8X4), rhs_scale=rows[1][:], start=True, stop=True)
             return bank[:].rearrange("p b q -> p (b q)")
 
@@ -94,45 +96,47 @@ def tile_attend_hvsaturating_twoheats_s_kernel(
         def blocks_of(tile):
             return [tile[:, b * P : (b + 1) * P] for b in range(BLOCKS)]
 
+        halves = [slice(0, HALF), slice(HALF, I)]
         offsets = sb.tile([P, I // 16], U16, name="offsets")
         nc.sync.dma_start(offsets[:], offs)
         q_raw = load_rows("q_raw", query, "rows_a")
         k_words = load_words("k_words", keys_words, "win_k")
-        k_scales = load_scales("k_scales", keys_scales, vec)
+        k_scales = load_scales("k_scales", keys_scales, act)
         half_win = load_row("half_win", halfp, "win_h", pool_eng)
         ceil_win = load_row("ceil_win", ceil_t, "win_c", vec)
         ident = sb.tile([P, P], F32, name="ident")
         make_identity(nc, ident[:])
-        v_scales = load_scales("v_scales", vals_scales, pool_eng)
+        v_scales = load_scales("v_scales", vals_scales, nc.sync)
         sharp_c = sb.tile([P, 1], F32, name="sharp_c")
         pool_eng.dma_start(out=sharp_c[:], in_=sharp)
         share_c = sb.tile([P, 1], F32, name="share_c")
         pool_eng.dma_start(out=share_c[:], in_=share)
 
-        k_bytes = gather("k_bytes", k_scales, U8)
+        k_bytes = gather("k_bytes", k_scales, U8, "k_bytes")
         q_mx = quantise("q", q_raw, act.copy)
         dq_raw = load_rows("dq_raw", dquery, "rows_a")
-        k_codes = gather("k_codes", k_words, U32)
-        a = scores_by_slot("a", q_mx, k_codes, k_bytes)
+        k_codes = gather("k_codes", k_words, U32, "k_codes", 2)
+        a = [scores_by_slot("a%d" % j, q_mx, k_codes, k_bytes, 2 * j, 2) for j in range(2)]
 
         half_row = wide("half_row")
         act.activation(out=half_row[:], in_=half_win[:].indirect(offsets[:]), func=ACT.Copy)
         half_turned = turn("half", half_row, "bank_g")
-        ceil_turned = turn("ceil", gather("ceil_row", ceil_win, F32), "bank_t")
-        v_words = load_words("v_words", vals_words, "win_h")
-        base_sb = sb.tile([P, T], F32, name="base_sb", tag="k_scales")
+        ceil_turned = turn("ceil", gather("ceil_row", ceil_win, F32, "ceil_row"), "bank_t")
+        v_words = load_words("v_words", vals_words, "k_scales")
+        base_sb = sb.tile([P, T], F32, name="base_sb", tag="win_c", align_bytes=64)
         nc.sync.dma_start(out=base_sb[:], in_=base)
-        placed = sb.tile([P, T], F32, name="placed", tag="win_k")
-        pool_eng.memset(placed[:], 0.0)
 
-        nth = wide("nth")
-        act.activation(out=nth[:], in_=a, func=ACT.Tanh, scale=-1.0)
+        nth = wide("nth", "win_h")
+        for j, cs in enumerate(halves):
+            act.activation(out=nth[:, cs], in_=a[j], func=ACT.Tanh, scale=-1.0)
         th_abs = wide("th_abs")
         vec.scalar_tensor_tensor(out=th_abs[:], in0=nth[:], scalar=-1.0, in1=nth[:], op0=ALU.mult, op1=ALU.max)
         lg = wide("lg")
-        act.activation(out=lg[:], in_=th_abs[:], func=ACT.Ln, scale=0.5, bias=0.5)
+        for cs in halves:
+            act.activation(out=lg[:, cs], in_=th_abs[:, cs], func=ACT.Ln, scale=0.5, bias=0.5)
         rl = wide("rl")
-        vec.tensor_scalar(out=rl[:], in0=a, scalar1=0.0, scalar2=None, op0=ALU.max)
+        for j, cs in enumerate(halves):
+            vec.tensor_scalar(out=rl[:, cs], in0=a[j], scalar1=0.0, scalar2=None, op0=ALU.max)
 
         hh = sb.tile([P, BLOCKS], F32, name="hh")
         cc = sb.tile([P, BLOCKS], F32, name="cc")
@@ -146,14 +150,18 @@ def tile_attend_hvsaturating_twoheats_s_kernel(
         vec.scalar_tensor_tensor(out=nkh[:], in0=cc[:], scalar=-0.5, in1=hh[:], op0=ALU.mult, op1=ALU.mult)
 
         fh = wide("fh")
-        vec.scalar_tensor_tensor(out=fh[:], in0=lg[:], scalar=-0.5, in1=rl[:], op0=ALU.mult, op1=ALU.add)
+        for cs in halves:
+            vec.scalar_tensor_tensor(out=fh[:, cs], in0=lg[:, cs], scalar=-0.5, in1=rl[:, cs], op0=ALU.mult, op1=ALU.add)
         y2 = wide("y2")
         for b in range(BLOCKS):
             act.activation(out=blocks_of(y2)[b], in_=blocks_of(fh)[b], func=ACT.Square, bias=hh[:, b : b + 1])
         ly = wide("ly")
         act.activation(out=ly[:], in_=y2[:], func=ACT.Ln)
         qq = wide("qq")
-        act.activation(out=qq[:], in_=ly[:], func=ACT.Exp, scale=-1.0)
+        for cs in halves:
+            act.activation(out=qq[:, cs], in_=ly[:, cs], func=ACT.Exp, scale=-1.0)
+        placed = sb.tile([P, T], F32, name="placed", tag="ly", align_bytes=64)
+        pool_eng.memset(placed[:], 0.0)
 
         s_bank = ps.tile([P, I], F32, name="s_bank")
         turn_into(s_bank, [cc[:, b : b + 1].to_broadcast([P, P]) for b in range(BLOCKS)], True, False)
@@ -161,15 +169,15 @@ def tile_attend_hvsaturating_twoheats_s_kernel(
         for b in range(BLOCKS):
             vec.tensor_scalar(out=blocks_of(nyk)[b], in0=blocks_of(fh)[b], scalar1=hh[:, b : b + 1], scalar2=nk[:, b : b + 1], op0=ALU.add, op1=ALU.mult)
         dq_mx = quantise("dq", dq_raw, vec.tensor_copy)
-        ta = scores_by_slot("ta", dq_mx, k_codes, k_bytes)
+        ta = scores_by_slot("ta", dq_mx, k_codes, k_bytes, 0, BLOCKS)
         pb1 = wide("pb1")
         vec.scalar_tensor_tensor(out=pb1[:], in0=nth[:], scalar=1.0, in1=ta, op0=ALU.add, op1=ALU.mult)
         f_bank = ps.tile([P, I], F32, name="f_bank")
         turn_into(f_bank, blocks_of(pb1), True, False)
         go_raw = load_rows("go_raw", gout, "rows_a")
         go_mx = quantise("go", go_raw, vec.tensor_copy)
-        v_bytes = gather("v_bytes", v_scales, U8)
-        v_codes = gather("v_codes", v_words, U32)
+        v_bytes = gather("v_bytes", v_scales, U8, "lg")
+        v_codes = gather("v_codes", v_words, U32, "rl")
         c0 = product("c0", go_mx, v_codes, v_bytes)
 
         cf = sb.tile([P, 3, 2], F32, name="cf")
@@ -177,8 +185,6 @@ def tile_attend_hvsaturating_twoheats_s_kernel(
         sh256 = sb.tile([P, 1], F32, name="sh256")
         pool_eng.tensor_scalar(out=shm1[:], in0=sharp_c[:], scalar1=-1.0, scalar2=1.0, op0=ALU.add, op1=ALU.mult)
         pool_eng.tensor_scalar(out=sh256[:], in0=share_c[:], scalar1=-1.0, scalar2=256.0, op0=ALU.add, op1=ALU.mult)
-        nsharp = sb.tile([P, 1], F32, name="nsharp")
-        pool_eng.tensor_scalar(out=nsharp[:], in0=sharp_c[:], scalar1=-1.0, scalar2=0.0, op0=ALU.mult, op1=ALU.add)
         for j in range(3):
             pool_eng.tensor_scalar(out=cf[:, j, 0:1], in0=share_c[:], scalar1=256.0, scalar2=0.0, op0=ALU.mult, op1=ALU.add)
         pool_eng.tensor_tensor(out=cf[:, 0, 1:2], in0=sh256[:], in1=sharp_c[:], op=ALU.mult)
@@ -187,8 +193,18 @@ def tile_attend_hvsaturating_twoheats_s_kernel(
         pool_eng.tensor_tensor(out=cf[:, 2, 1:2], in0=cf[:, 0, 1:2], in1=shm1[:], op=ALU.mult)
 
         nv = wide("nv")
-        vec.tensor_tensor(out=nv[:], in0=nyk[:], in1=qq[:], op=ALU.mult)
+        for cs in halves:
+            vec.tensor_tensor(out=nv[:, cs], in0=nyk[:, cs], in1=qq[:, cs], op=ALU.mult)
         turn_into(s_bank, blocks_of(nv), False, True)
+        low = sb.tile([P, 2], F32, name="low")
+        ns = [wide("ns1"), wide("ns2")]
+        vec.tensor_scalar(out=ns[0][:], in0=s_bank[:], scalar1=-1.0, scalar2=None, op0=ALU.mult, op1=ALU.min, accum_out=low[:, 0:1])
+        vec.tensor_scalar(out=ns[1][:], in0=ns[0][:], scalar1=sharp_c[:], scalar2=None, op0=ALU.mult, op1=ALU.min, accum_out=low[:, 1:2])
+        z = sb.tile([P, 2], F32, name="z")
+        p = [wide("p1"), wide("p2")]
+        for h in range(2):
+            act.activation(out=p[h][:], in_=ns[h][:], func=ACT.Exp, scale=-1.0, bias=low[:, h : h + 1], accum_out=z[:, h : h + 1])
+
         gq = wide("gq")
         vec.scalar_tensor_tensor(out=gq[:], in0=nth[:], scalar=-1.0, in1=qq[:], op0=ALU.add, op1=ALU.mult)
         tq = wide("tq")
@@ -196,17 +212,10 @@ def tile_attend_hvsaturating_twoheats_s_kernel(
         tst = wide("tst")
         for b in range(BLOCKS):
             act.activation(out=blocks_of(tst)[b], in_=blocks_of(tq)[b], func=ACT.Copy, scale=nkh[:, b : b + 1])
-        low = sb.tile([P, 2], F32, name="low")
-        vec.tensor_reduce(out=low[:, 0:1], in_=s_bank[:], axis=mybir.AxisListType.X, op=ALU.max, negate=True)
-        ns2 = wide("ns2")
-        vec.tensor_scalar(out=ns2[:], in0=s_bank[:], scalar1=nsharp[:], scalar2=None, op0=ALU.mult, op1=ALU.min, accum_out=low[:, 1:2])
-        z = sb.tile([P, 2], F32, name="z")
-        p = [wide("p1"), wide("p2")]
-        act.activation(out=p[0][:], in_=s_bank[:], func=ACT.Exp, bias=low[:, 0:1], accum_out=z[:, 0:1])
-        act.activation(out=p[1][:], in_=ns2[:], func=ACT.Exp, scale=-1.0, bias=low[:, 1:2], accum_out=z[:, 1:2])
-
         ts = ps.tile([P, I], F32, name="ts", tag="bank_t")
         turn_into(ts, blocks_of(tst), True, True)
+        ts_again = ps.tile([P, I], F32, name="ts_again", tag="a0")
+        turn_into(ts_again, blocks_of(tst), True, True)
         dqq = wide("dqq")
         for b in range(BLOCKS):
             vec.scalar_tensor_tensor(out=blocks_of(dqq)[b], in0=blocks_of(fh)[b], scalar=c3[:, b : b + 1], in1=blocks_of(tq)[b], op0=ALU.add, op1=ALU.mult)
@@ -216,42 +225,40 @@ def tile_attend_hvsaturating_twoheats_s_kernel(
             act.activation(out=blocks_of(g4t)[b], in_=blocks_of(gq)[b], func=ACT.Copy, scale=nk[:, b : b + 1])
         g_bank = ps.tile([P, I], F32, name="g_bank", tag="bank_g")
         turn_into(g_bank, blocks_of(g4t), True, True)
-        rz = sb.tile([P, 2], F32, name="rz")
-        vec.reciprocal(out=rz[:], in_=z[:])
-        aa = sb.tile([P, 3, 2], F32, name="aa")
-        vec.tensor_tensor(out=aa[:], in0=cf[:], in1=rz[:].unsqueeze(1).to_broadcast([P, 3, 2]), op=ALU.mult)
-        c1 = sb.tile([P, 2], F32, name="c1")
-        vec.scalar_tensor_tensor(out=c1[:], in0=aa[:, 1, :], scalar=-1.0, in1=rz[:], op0=ALU.mult, op1=ALU.mult)
 
+        rz = sb.tile([P, 2], F32, name="rz")
+        aa = sb.tile([P, 3, 2], F32, name="aa")
+        c1 = sb.tile([P, 2], F32, name="c1")
         tb = sb.tile([P, 2], F32, name="tb")
+        msum = sb.tile([P, 2], F32, name="msum")
         m = sb.tile([P, 2], F32, name="m")
         nn = sb.tile([P, 2], F32, name="nn")
         ak = sb.tile([P, 2], F32, name="ak")
         f = [wide("ff1"), wide("ff2")]
-        rc = [wide("rc1"), wide("rc2")]
+        pc = [wide("pc1"), wide("pc2")]
+
+        def summed(dst, x, factor, y, total):
+            vec.scalar_tensor_tensor(out=dst[:], in0=x[:], scalar=factor, in1=y[:], op0=ALU.mult, op1=ALU.mult, accum_out=total)
+
+        vec.reciprocal(out=rz[:], in_=z[:])
+        summed(pc[0], p[0], -1.0, c0, msum[:, 0:1])
+        vec.tensor_tensor(out=aa[:], in0=cf[:], in1=rz[:].unsqueeze(1).to_broadcast([P, 3, 2]), op=ALU.mult)
+        summed(pc[1], p[1], -1.0, c0, msum[:, 1:2])
+        vec.scalar_tensor_tensor(out=c1[:], in0=aa[:, 1, :], scalar=-1.0, in1=rz[:], op0=ALU.mult, op1=ALU.mult)
+        vec.scalar_tensor_tensor(out=m[:], in0=msum[:], scalar=-1.0, in1=rz[:], op0=ALU.mult, op1=ALU.mult)
         for h in (1, 0):
-            col = slice(h, h + 1)
-            junk = wide("junk_t%d" % h)
-            vec.scalar_tensor_tensor(out=junk[:], in0=p[h][:], scalar=c1[:, col], in1=ts[:], op0=ALU.mult, op1=ALU.mult, accum_out=tb[:, col])
+            summed(wide("spent_t%d" % h), p[h], c1[:, h : h + 1], ts, tb[:, h : h + 1])
         f2a = wide("f2a")
-        act.activation(out=f2a[:], in_=ts[:], func=ACT.Identity, scale=aa[:, 2, 1:2], bias=tb[:, 1:2])
+        act.activation(out=f2a[:], in_=ts_again[:], func=ACT.Identity, scale=aa[:, 2, 1:2], bias=tb[:, 1:2])
         act.activation(out=f[0][:], in_=f_bank[:], func=ACT.Identity, scale=aa[:, 0, 0:1], bias=tb[:, 0:1])
+        for h in range(2):
+            col = slice(h, h + 1)
+            summed(wide("spent_n%d" % h), pc[h], c1[:, col], ts, nn[:, col])
+            act.activation(out=ak[:, col], in_=tb[:, col], func=ACT.Identity, scale=m[:, col], bias=nn[:, col])
         g4 = wide("g4")
         act.copy(out=g4[:], in_=g_bank[:])
-        for h in range(2):
-            col = slice(h, h + 1)
-            vec.scalar_tensor_tensor(out=rc[h][:], in0=p[h][:], scalar=rz[:, col], in1=c0[:], op0=ALU.mult, op1=ALU.mult, accum_out=m[:, col])
-        for h in range(2):
-            col = slice(h, h + 1)
-            junk = wide("junk_n%d" % h)
-            vec.scalar_tensor_tensor(out=junk[:], in0=rc[h][:], scalar=aa[:, 1, col], in1=ts[:], op0=ALU.mult, op1=ALU.mult, accum_out=nn[:, col])
-            act.activation(out=ak[:, col], in_=tb[:, col], func=ACT.Identity, scale=m[:, col], bias=nn[:, col])
-
         vec.scalar_tensor_tensor(out=f[1][:], in0=f_bank[:], scalar=aa[:, 0, 1:2], in1=f2a[:], op0=ALU.mult, op1=ALU.add)
 
-        probe = sb.tile([P, 4], F32, name="probe")
-        pool_eng.tensor_copy(out=probe[:, 0:1], in_=qq[:, 0:1])
-        pool_eng.tensor_copy(out=probe[:, 1:2], in_=tb[:, 0:1])
         for part in range(2):
             cs = slice(part * HALF, (part + 1) * HALF)
             picks = offsets[:, part * (HALF // 16) : (part + 1) * (HALF // 16)]

@@ -18,7 +18,7 @@ ACT = mybir.ActivationFunctionType
 P = 128
 BLOCKS = I // P
 HALF = I // 2
-CHUNK = 512
+EDGES = (0, 640, 1280, 1792, 2048)
 
 
 def tile_attend_hvsaturating_twoheats_s_kernel(
@@ -33,22 +33,22 @@ def tile_attend_hvsaturating_twoheats_s_kernel(
         def wide(name, tag=None):
             return sb.tile([P, I], F32, name=name, tag=tag or name, align_bytes=64)
 
-        def load_scales(name, scales, queue):
-            tile = sb.tile([P, T], U8, name=name, tag=name, align_bytes=64)
-            pool_eng.memset(tile[:].bitcast(I32), 0)
+        def load_scales(name, scales, zeroer):
+            tile = sb.tile([P, T + 4], U8, name=name, tag=name, align_bytes=64)
+            zeroer.memset(tile[:].bitcast(I32), 0)
             for quad in range(4):
-                queue.dma_start(out=tile[32 * quad : 32 * quad + 4, 0:T].bitcast(I32), in_=scales[0, 4 * quad : 4 * quad + 4, :].bitcast(I32))
+                nc.sync.dma_start(out=tile[32 * quad : 32 * quad + 4, 0:T].bitcast(I32), in_=scales[0, 4 * quad : 4 * quad + 4, :].bitcast(I32))
             return tile
 
-        def load_words(name, words, tag):
+        def load_words(name, words, tag, queue):
             tile = sb.tile([P, T], U32, name=name, tag=tag, align_bytes=64)
-            nc.sync.dma_start(out=tile[:].bitcast(I32), in_=words[0].rearrange("p n t -> p (n t)").bitcast(I32))
+            queue.dma_start(out=tile[:].bitcast(I32), in_=words[0].rearrange("p n t -> p (n t)").bitcast(I32))
             return tile
 
-        def load_row(name, table, tag, zeroer):
+        def load_row(name, table, tag, zeroer, row):
             tile = sb.tile([P, T + 1], F32, name=name, tag=tag, align_bytes=64)
             zeroer.memset(tile[:], 0.0)
-            nc.sync.dma_start(out=tile[0:1, 0:T], in_=table[0:1, :])
+            nc.sync.dma_start(out=tile[row : row + 1, 0:T], in_=table[0:1, :])
             return tile
 
         def load_rows(name, rows, tag):
@@ -56,8 +56,11 @@ def tile_attend_hvsaturating_twoheats_s_kernel(
             nc.sync.dma_start(out=raw[:], in_=rows.rearrange("(p j) w -> p j w", j=4))
             return raw
 
-        def quantise(name, raw, cast):
-            grouped = sb.tile([P, Q, 4], BF16, name=name + "_bf", align_bytes=64)
+        def scalar_cast(out, in_):
+            act.activation(out=out, in_=in_, func=ACT.Copy)
+
+        def quantise(name, raw, cast, tag):
+            grouped = sb.tile([P, Q, 4], BF16, name=name + "_bf", tag=tag, align_bytes=64)
             cast(out=grouped[:], in_=raw[:].rearrange("p j w -> p w j"))
             codes = sb.tile([P, Q], U32, name=name + "_codes", align_bytes=64)
             scales = sb.tile([P, Q], U8, name=name + "_scales", align_bytes=64)
@@ -74,12 +77,6 @@ def tile_attend_hvsaturating_twoheats_s_kernel(
         def product(name, rows, words, scales):
             bank = ps.tile([P, I], F32, name=name)
             pe.matmul_mx(out=bank[:], lhsT=rows[0][:].bitcast(FP8X4), lhsT_scale=rows[1][:], rhs=words[:].bitcast(FP8X4), rhs_scale=scales[:], start=True, stop=True)
-            return bank
-
-        def turn(name, picked, tag):
-            bank = ps.tile([P, BLOCKS, P], F32, name=name + "_turned", tag=tag)
-            for b in range(BLOCKS):
-                pe.transpose(bank[:, b, :], picked[:, b * P : (b + 1) * P], ident[:])
             return bank
 
         def scores_by_slot(name, rows, words, scales, first, count):
@@ -100,33 +97,34 @@ def tile_attend_hvsaturating_twoheats_s_kernel(
         offsets = sb.tile([P, I // 16], U16, name="offsets")
         nc.sync.dma_start(offsets[:], offs)
         q_raw = load_rows("q_raw", query, "rows_a")
-        k_words = load_words("k_words", keys_words, "win_k")
-        k_scales = load_scales("k_scales", keys_scales, act)
-        half_win = load_row("half_win", halfp, "win_h", pool_eng)
-        ceil_win = load_row("ceil_win", ceil_t, "win_c", vec)
+        k_words = load_words("k_words", keys_words, "win_k", act)
+        k_scales = load_scales("k_scales", keys_scales, vec)
+        half_win = load_row("half_win", halfp, "win_h", pool_eng, 0)
+        ceil_win = load_row("ceil_win", ceil_t, "win_c", vec, 1)
         ident = sb.tile([P, P], F32, name="ident")
         make_identity(nc, ident[:])
-        v_scales = load_scales("v_scales", vals_scales, nc.sync)
+        v_scales = load_scales("v_scales", vals_scales, pool_eng)
         sharp_c = sb.tile([P, 1], F32, name="sharp_c")
         pool_eng.dma_start(out=sharp_c[:], in_=sharp)
         share_c = sb.tile([P, 1], F32, name="share_c")
         pool_eng.dma_start(out=share_c[:], in_=share)
 
         k_bytes = gather("k_bytes", k_scales, U8, "k_bytes")
-        q_mx = quantise("q", q_raw, act.copy)
+        q_mx = quantise("q", q_raw, scalar_cast, "q_bf")
         dq_raw = load_rows("dq_raw", dquery, "rows_a")
         k_codes = gather("k_codes", k_words, U32, "k_codes", 2)
         a = [scores_by_slot("a%d" % j, q_mx, k_codes, k_bytes, 2 * j, 2) for j in range(2)]
 
-        half_row = wide("half_row")
-        act.activation(out=half_row[:], in_=half_win[:].indirect(offsets[:]), func=ACT.Copy)
-        half_turned = turn("half", half_row, "bank_g")
-        ceil_turned = turn("ceil", gather("ceil_row", ceil_win, F32, "ceil_row"), "bank_t")
-        v_words = load_words("v_words", vals_words, "k_scales")
-        base_sb = sb.tile([P, T], F32, name="base_sb", tag="win_c", align_bytes=64)
+        turned = ps.tile([P, I], F32, name="turned", tag="bank_g")
+        for j, window in enumerate((half_win, ceil_win)):
+            picked = wide("picked%d" % j)
+            act.activation(out=picked[:], in_=window[:].indirect(offsets[:]), func=ACT.Copy)
+            turn_into(turned, blocks_of(picked), j == 0, j == 1)
+        v_words = load_words("v_words", vals_words, "k_scales", nc.sync)
+        base_sb = sb.tile([P, T], F32, name="base_sb", tag="win_h", align_bytes=64)
         nc.sync.dma_start(out=base_sb[:], in_=base)
 
-        nth = wide("nth", "win_h")
+        nth = wide("nth", "win_c")
         for j, cs in enumerate(halves):
             act.activation(out=nth[:, cs], in_=a[j], func=ACT.Tanh, scale=-1.0)
         th_abs = wide("th_abs")
@@ -136,22 +134,19 @@ def tile_attend_hvsaturating_twoheats_s_kernel(
             act.activation(out=lg[:, cs], in_=th_abs[:, cs], func=ACT.Ln, scale=0.5, bias=0.5)
         rl = wide("rl")
         for j, cs in enumerate(halves):
-            vec.tensor_scalar(out=rl[:, cs], in0=a[j], scalar1=0.0, scalar2=None, op0=ALU.max)
+            vec.tensor_scalar(out=rl[:, cs], in0=a[j], scalar1=0.0, scalar2=2.0, op0=ALU.max, op1=ALU.mult)
 
-        hh = sb.tile([P, BLOCKS], F32, name="hh")
-        cc = sb.tile([P, BLOCKS], F32, name="cc")
+        hc = sb.tile([P, 2, BLOCKS], F32, name="hc")
         nk = sb.tile([P, BLOCKS], F32, name="nk")
         c3 = sb.tile([P, BLOCKS], F32, name="c3")
-        vec.tensor_scalar(out=hh[:], in0=half_turned[:, :, 0], scalar1=0.5, scalar2=None, op0=ALU.mult)
-        vec.tensor_copy(out=cc[:], in_=ceil_turned[:, :, 0])
-        vec.scalar_tensor_tensor(out=nk[:], in0=cc[:], scalar=-1.0, in1=hh[:], op0=ALU.mult, op1=ALU.mult)
-        vec.scalar_tensor_tensor(out=c3[:], in0=nk[:], scalar=0.5, in1=hh[:], op0=ALU.mult, op1=ALU.add)
-        nkh = sb.tile([P, BLOCKS], F32, name="nkh")
-        vec.scalar_tensor_tensor(out=nkh[:], in0=cc[:], scalar=-0.5, in1=hh[:], op0=ALU.mult, op1=ALU.mult)
+        vec.tensor_copy(out=hc[:], in_=turned[:].rearrange("p (b q) -> p q b", b=BLOCKS)[:, 0:2, :])
+        hh, cc = hc[:, 0, :], hc[:, 1, :]
+        vec.scalar_tensor_tensor(out=nk[:], in0=cc, scalar=-1.0, in1=hh, op0=ALU.mult, op1=ALU.mult)
+        vec.scalar_tensor_tensor(out=c3[:], in0=nk[:], scalar=0.5, in1=hh, op0=ALU.mult, op1=ALU.add)
 
         fh = wide("fh")
         for cs in halves:
-            vec.scalar_tensor_tensor(out=fh[:, cs], in0=lg[:, cs], scalar=-0.5, in1=rl[:, cs], op0=ALU.mult, op1=ALU.add)
+            vec.tensor_tensor(out=fh[:, cs], in0=rl[:, cs], in1=lg[:, cs], op=ALU.subtract)
         y2 = wide("y2")
         for b in range(BLOCKS):
             act.activation(out=blocks_of(y2)[b], in_=blocks_of(fh)[b], func=ACT.Square, bias=hh[:, b : b + 1])
@@ -168,14 +163,14 @@ def tile_attend_hvsaturating_twoheats_s_kernel(
         nyk = wide("nyk")
         for b in range(BLOCKS):
             vec.tensor_scalar(out=blocks_of(nyk)[b], in0=blocks_of(fh)[b], scalar1=hh[:, b : b + 1], scalar2=nk[:, b : b + 1], op0=ALU.add, op1=ALU.mult)
-        dq_mx = quantise("dq", dq_raw, vec.tensor_copy)
+        dq_mx = quantise("dq", dq_raw, vec.tensor_copy, "dq_bf")
         ta = scores_by_slot("ta", dq_mx, k_codes, k_bytes, 0, BLOCKS)
         pb1 = wide("pb1")
         vec.scalar_tensor_tensor(out=pb1[:], in0=nth[:], scalar=1.0, in1=ta, op0=ALU.add, op1=ALU.mult)
         f_bank = ps.tile([P, I], F32, name="f_bank")
         turn_into(f_bank, blocks_of(pb1), True, False)
         go_raw = load_rows("go_raw", gout, "rows_a")
-        go_mx = quantise("go", go_raw, vec.tensor_copy)
+        go_mx = quantise("go", go_raw, scalar_cast, "y2")
         v_bytes = gather("v_bytes", v_scales, U8, "lg")
         v_codes = gather("v_codes", v_words, U32, "rl")
         c0 = product("c0", go_mx, v_codes, v_bytes)
@@ -184,13 +179,12 @@ def tile_attend_hvsaturating_twoheats_s_kernel(
         shm1 = sb.tile([P, 1], F32, name="shm1")
         sh256 = sb.tile([P, 1], F32, name="sh256")
         pool_eng.tensor_scalar(out=shm1[:], in0=sharp_c[:], scalar1=-1.0, scalar2=1.0, op0=ALU.add, op1=ALU.mult)
-        pool_eng.tensor_scalar(out=sh256[:], in0=share_c[:], scalar1=-1.0, scalar2=256.0, op0=ALU.add, op1=ALU.mult)
-        for j in range(3):
-            pool_eng.tensor_scalar(out=cf[:, j, 0:1], in0=share_c[:], scalar1=256.0, scalar2=0.0, op0=ALU.mult, op1=ALU.add)
-        pool_eng.tensor_tensor(out=cf[:, 0, 1:2], in0=sh256[:], in1=sharp_c[:], op=ALU.mult)
-        pool_eng.tensor_tensor(out=cf[:, 1, 1:2], in0=cf[:, 0, 1:2], in1=sharp_c[:], op=ALU.mult)
-
-        pool_eng.tensor_tensor(out=cf[:, 2, 1:2], in0=cf[:, 0, 1:2], in1=shm1[:], op=ALU.mult)
+        pool_eng.tensor_scalar(out=sh256[:], in0=share_c[:], scalar1=-1.0, scalar2=sharp_c[:], op0=ALU.add, op1=ALU.mult)
+        for j, factor in enumerate((512.0, 256.0, 0.0)):
+            pool_eng.tensor_scalar(out=cf[:, j, 0:1], in0=share_c[:], scalar1=factor, scalar2=0.0, op0=ALU.mult, op1=ALU.add)
+        pool_eng.tensor_scalar(out=cf[:, 0, 1:2], in0=sh256[:], scalar1=512.0, scalar2=0.0, op0=ALU.mult, op1=ALU.add)
+        pool_eng.tensor_scalar(out=cf[:, 1, 1:2], in0=sh256[:], scalar1=256.0, scalar2=sharp_c[:], op0=ALU.mult, op1=ALU.mult)
+        pool_eng.tensor_scalar(out=cf[:, 2, 1:2], in0=sh256[:], scalar1=256.0, scalar2=shm1[:], op0=ALU.mult, op1=ALU.mult)
 
         nv = wide("nv")
         for cs in halves:
@@ -208,11 +202,11 @@ def tile_attend_hvsaturating_twoheats_s_kernel(
         gq = wide("gq")
         vec.scalar_tensor_tensor(out=gq[:], in0=nth[:], scalar=-1.0, in1=qq[:], op0=ALU.add, op1=ALU.mult)
         tq = wide("tq")
-        vec.tensor_tensor(out=tq[:], in0=ta, in1=gq[:], op=ALU.mult)
+        vec.scalar_tensor_tensor(out=tq[:], in0=ta, scalar=2.0, in1=gq[:], op0=ALU.mult, op1=ALU.mult)
         tst = wide("tst")
         for b in range(BLOCKS):
-            act.activation(out=blocks_of(tst)[b], in_=blocks_of(tq)[b], func=ACT.Copy, scale=nkh[:, b : b + 1])
-        ts = ps.tile([P, I], F32, name="ts", tag="bank_t")
+            act.activation(out=blocks_of(tst)[b], in_=blocks_of(tq)[b], func=ACT.Copy, scale=nk[:, b : b + 1])
+        ts = ps.tile([P, I], F32, name="ts")
         turn_into(ts, blocks_of(tst), True, True)
         ts_again = ps.tile([P, I], F32, name="ts_again", tag="a0")
         turn_into(ts_again, blocks_of(tst), True, True)
@@ -225,12 +219,14 @@ def tile_attend_hvsaturating_twoheats_s_kernel(
             act.activation(out=blocks_of(g4t)[b], in_=blocks_of(gq)[b], func=ACT.Copy, scale=nk[:, b : b + 1])
         g_bank = ps.tile([P, I], F32, name="g_bank", tag="bank_g")
         turn_into(g_bank, blocks_of(g4t), True, True)
+        g4 = wide("g4")
+        act.copy(out=g4[:], in_=g_bank[:])
 
         rz = sb.tile([P, 2], F32, name="rz")
         aa = sb.tile([P, 3, 2], F32, name="aa")
         c1 = sb.tile([P, 2], F32, name="c1")
         tb = sb.tile([P, 2], F32, name="tb")
-        msum = sb.tile([P, 2], F32, name="msum")
+        msum = sb.tile([P, 2], F32, name="msum", tag="msum", align_bytes=64)
         m = sb.tile([P, 2], F32, name="m")
         nn = sb.tile([P, 2], F32, name="nn")
         ak = sb.tile([P, 2], F32, name="ak")
@@ -246,6 +242,9 @@ def tile_attend_hvsaturating_twoheats_s_kernel(
         summed(pc[1], p[1], -1.0, c0, msum[:, 1:2])
         vec.scalar_tensor_tensor(out=c1[:], in0=aa[:, 1, :], scalar=-1.0, in1=rz[:], op0=ALU.mult, op1=ALU.mult)
         vec.scalar_tensor_tensor(out=m[:], in0=msum[:], scalar=-1.0, in1=rz[:], op0=ALU.mult, op1=ALU.mult)
+        pg = [wide("pg1", "msum"), wide("pg2")]
+        for h in range(2):
+            pool_eng.tensor_tensor(out=pg[h][:], in0=p[h][:], in1=g4[:], op=ALU.mult)
         for h in (1, 0):
             summed(wide("spent_t%d" % h), p[h], c1[:, h : h + 1], ts, tb[:, h : h + 1])
         f2a = wide("f2a")
@@ -255,8 +254,6 @@ def tile_attend_hvsaturating_twoheats_s_kernel(
             col = slice(h, h + 1)
             summed(wide("spent_n%d" % h), pc[h], c1[:, col], ts, nn[:, col])
             act.activation(out=ak[:, col], in_=tb[:, col], func=ACT.Identity, scale=m[:, col], bias=nn[:, col])
-        g4 = wide("g4")
-        act.copy(out=g4[:], in_=g_bank[:])
         vec.scalar_tensor_tensor(out=f[1][:], in0=f_bank[:], scalar=aa[:, 0, 1:2], in1=f2a[:], op0=ALU.mult, op1=ALU.add)
 
         for part in range(2):
@@ -267,18 +264,16 @@ def tile_attend_hvsaturating_twoheats_s_kernel(
             for h in range(2):
                 vec.scalar_tensor_tensor(out=b[h][:], in0=c0[:, cs], scalar=m[:, h : h + 1], in1=f[h][:, cs], op0=ALU.subtract, op1=ALU.mult)
             for h in range(2):
-                vec.scalar_tensor_tensor(out=o[h][:], in0=b[h][:], scalar=ak[:, h : h + 1], in1=p[h][:, cs], op0=ALU.subtract, op1=ALU.mult)
-            both = sb.tile([P, HALF], F32, name="both%d" % part)
-            vec.tensor_tensor(out=both[:], in0=o[0][:], in1=o[1][:], op=ALU.add)
+                vec.scalar_tensor_tensor(out=o[h][:], in0=b[h][:], scalar=ak[:, h : h + 1], in1=pg[h][:, cs], op0=ALU.subtract, op1=ALU.mult)
             if part == 0:
                 gs = sb.tile([P, HALF], F32, name="gs")
-                vec.tensor_tensor(out=gs[:], in0=both[:], in1=g4[:, cs], op=ALU.mult)
+                vec.tensor_tensor(out=gs[:], in0=o[0][:], in1=o[1][:], op=ALU.add)
                 act.activation(out=placed[:].indirect(picks), in_=gs[:], func=ACT.Copy)
             else:
-                vec.tensor_tensor(out=placed[:].indirect(picks), in0=both[:], in1=g4[:, cs], op=ALU.mult)
+                vec.tensor_tensor(out=placed[:].indirect(picks), in0=o[0][:], in1=o[1][:], op=ALU.add)
 
-        for c in range(T // CHUNK):
-            cs = slice(c * CHUNK, (c + 1) * CHUNK)
-            res = sb.tile([P, CHUNK], F32, name="res%d" % c)
+        for c in range(len(EDGES) - 1):
+            cs = slice(EDGES[c], EDGES[c + 1])
+            res = sb.tile([P, EDGES[c + 1] - EDGES[c]], F32, name="res%d" % c)
             vec.tensor_tensor(out=res[:], in0=placed[:, cs], in1=base_sb[:, cs], op=ALU.add)
             nc.sync.dma_start(out=out[:, cs], in_=res[:])

@@ -18,7 +18,7 @@ ACT = mybir.ActivationFunctionType
 P = 128
 BLOCKS = I // P
 HALF = I // 2
-EDGES = (0, 640, 1280, 1792, 2048)
+EDGES = (0, 512, 1024, 1408)
 
 
 def tile_attend_hvsaturating_twoheats_s_kernel(
@@ -87,8 +87,8 @@ def tile_attend_hvsaturating_twoheats_s_kernel(
             return bank[:].rearrange("p b q -> p (b q)")
 
         def turn_into(bank, blocks, first, last):
-            for b in range(BLOCKS):
-                pe.matmul(out=bank[:, b * P : (b + 1) * P], lhsT=blocks[b], rhs=ident[:], is_transpose=True, start=first and b == 0, stop=last and b == BLOCKS - 1)
+            for b, block in enumerate(blocks):
+                pe.matmul(out=bank[:, b * P : (b + 1) * P], lhsT=block, rhs=ident[:], is_transpose=True, start=first and b == 0, stop=last and b == len(blocks) - 1)
 
         def blocks_of(tile):
             return [tile[:, b * P : (b + 1) * P] for b in range(BLOCKS)]
@@ -111,6 +111,8 @@ def tile_attend_hvsaturating_twoheats_s_kernel(
 
         k_bytes = gather("k_bytes", k_scales, U8, "k_bytes")
         q_mx = quantise("q", q_raw, scalar_cast, "q_bf")
+        placed = sb.tile([P, T], F32, name="placed", tag="q_bf", align_bytes=64)
+        pool_eng.memset(placed[:], 0.0)
         dq_raw = load_rows("dq_raw", dquery, "rows_a")
         k_codes = gather("k_codes", k_words, U32, "k_codes", 2)
         a = [scores_by_slot("a%d" % j, q_mx, k_codes, k_bytes, 2 * j, 2) for j in range(2)]
@@ -118,7 +120,7 @@ def tile_attend_hvsaturating_twoheats_s_kernel(
         turned = ps.tile([P, I], F32, name="turned", tag="bank_g")
         for j, window in enumerate((half_win, ceil_win)):
             picked = wide("picked%d" % j)
-            act.activation(out=picked[:], in_=window[:].indirect(offsets[:]), func=ACT.Copy)
+            scalar_cast(out=picked[:], in_=window[:].indirect(offsets[:]))
             turn_into(turned, blocks_of(picked), j == 0, j == 1)
         v_words = load_words("v_words", vals_words, "k_scales", nc.sync)
         base_sb = sb.tile([P, T], F32, name="base_sb", tag="win_h", align_bytes=64)
@@ -155,14 +157,15 @@ def tile_attend_hvsaturating_twoheats_s_kernel(
         qq = wide("qq")
         for cs in halves:
             act.activation(out=qq[:, cs], in_=ly[:, cs], func=ACT.Exp, scale=-1.0)
-        placed = sb.tile([P, T], F32, name="placed", tag="ly", align_bytes=64)
-        pool_eng.memset(placed[:], 0.0)
 
-        s_bank = ps.tile([P, I], F32, name="s_bank")
+        s_bank = ps.tile([P, I], F32, name="s_bank", tag="s_bank")
         turn_into(s_bank, [cc[:, b : b + 1].to_broadcast([P, P]) for b in range(BLOCKS)], True, False)
         nyk = wide("nyk")
         for b in range(BLOCKS):
-            vec.tensor_scalar(out=blocks_of(nyk)[b], in0=blocks_of(fh)[b], scalar1=hh[:, b : b + 1], scalar2=nk[:, b : b + 1], op0=ALU.add, op1=ALU.mult)
+            pool_eng.tensor_scalar(out=blocks_of(nyk)[b], in0=blocks_of(fh)[b], scalar1=hh[:, b : b + 1], scalar2=nk[:, b : b + 1], op0=ALU.add, op1=ALU.mult)
+        fc = wide("fc", "y2")
+        for b in range(BLOCKS):
+            act.activation(out=blocks_of(fc)[b], in_=blocks_of(fh)[b], func=ACT.Identity, bias=c3[:, b : b + 1])
         dq_mx = quantise("dq", dq_raw, vec.tensor_copy, "dq_bf")
         ta = scores_by_slot("ta", dq_mx, k_codes, k_bytes, 0, BLOCKS)
         pb1 = wide("pb1")
@@ -170,21 +173,20 @@ def tile_attend_hvsaturating_twoheats_s_kernel(
         f_bank = ps.tile([P, I], F32, name="f_bank")
         turn_into(f_bank, blocks_of(pb1), True, False)
         go_raw = load_rows("go_raw", gout, "rows_a")
-        go_mx = quantise("go", go_raw, scalar_cast, "y2")
+        go_mx = quantise("go", go_raw, scalar_cast, "ly")
         v_bytes = gather("v_bytes", v_scales, U8, "lg")
         v_codes = gather("v_codes", v_words, U32, "rl")
         c0 = product("c0", go_mx, v_codes, v_bytes)
 
-        cf = sb.tile([P, 3, 2], F32, name="cf")
+        cf = sb.tile([P, 2, 4], F32, name="cf")
         shm1 = sb.tile([P, 1], F32, name="shm1")
-        sh256 = sb.tile([P, 1], F32, name="sh256")
+        beta = sb.tile([P, 1], F32, name="beta")
         pool_eng.tensor_scalar(out=shm1[:], in0=sharp_c[:], scalar1=-1.0, scalar2=1.0, op0=ALU.add, op1=ALU.mult)
-        pool_eng.tensor_scalar(out=sh256[:], in0=share_c[:], scalar1=-1.0, scalar2=sharp_c[:], op0=ALU.add, op1=ALU.mult)
-        for j, factor in enumerate((512.0, 256.0, 0.0)):
-            pool_eng.tensor_scalar(out=cf[:, j, 0:1], in0=share_c[:], scalar1=factor, scalar2=0.0, op0=ALU.mult, op1=ALU.add)
-        pool_eng.tensor_scalar(out=cf[:, 0, 1:2], in0=sh256[:], scalar1=512.0, scalar2=0.0, op0=ALU.mult, op1=ALU.add)
-        pool_eng.tensor_scalar(out=cf[:, 1, 1:2], in0=sh256[:], scalar1=256.0, scalar2=sharp_c[:], op0=ALU.mult, op1=ALU.mult)
-        pool_eng.tensor_scalar(out=cf[:, 2, 1:2], in0=sh256[:], scalar1=256.0, scalar2=shm1[:], op0=ALU.mult, op1=ALU.mult)
+        pool_eng.tensor_scalar(out=beta[:], in0=share_c[:], scalar1=-1.0, scalar2=sharp_c[:], op0=ALU.add, op1=ALU.mult)
+        for j, factor in enumerate((512.0, 0.0, 256.0, -256.0)):
+            pool_eng.tensor_scalar(out=cf[:, 0, j : j + 1], in0=share_c[:], scalar1=factor, scalar2=1.0, op0=ALU.mult, op1=ALU.mult)
+        for j, (factor, other) in enumerate(((512.0, 1.0), (256.0, shm1[:]), (256.0, sharp_c[:]), (-256.0, sharp_c[:]))):
+            pool_eng.tensor_scalar(out=cf[:, 1, j : j + 1], in0=beta[:], scalar1=factor, scalar2=other, op0=ALU.mult, op1=ALU.mult)
 
         nv = wide("nv")
         for cs in halves:
@@ -211,54 +213,68 @@ def tile_attend_hvsaturating_twoheats_s_kernel(
         ts_again = ps.tile([P, I], F32, name="ts_again", tag="a0")
         turn_into(ts_again, blocks_of(tst), True, True)
         dqq = wide("dqq")
-        for b in range(BLOCKS):
-            vec.scalar_tensor_tensor(out=blocks_of(dqq)[b], in0=blocks_of(fh)[b], scalar=c3[:, b : b + 1], in1=blocks_of(tq)[b], op0=ALU.add, op1=ALU.mult)
+        pool_eng.tensor_tensor(out=dqq[:], in0=fc[:], in1=tq[:], op=ALU.mult)
         turn_into(f_bank, blocks_of(dqq), False, True)
         g4t = wide("g4t")
         for b in range(BLOCKS):
             act.activation(out=blocks_of(g4t)[b], in_=blocks_of(gq)[b], func=ACT.Copy, scale=nk[:, b : b + 1])
         g_bank = ps.tile([P, I], F32, name="g_bank", tag="bank_g")
         turn_into(g_bank, blocks_of(g4t), True, True)
-        g4 = wide("g4")
-        act.copy(out=g4[:], in_=g_bank[:])
 
         rz = sb.tile([P, 2], F32, name="rz")
-        aa = sb.tile([P, 3, 2], F32, name="aa")
-        c1 = sb.tile([P, 2], F32, name="c1")
+        aa = sb.tile([P, 2, 4], F32, name="aa")
+        c1 = sb.tile([P, 2, 2], F32, name="c1")
         tb = sb.tile([P, 2], F32, name="tb")
-        msum = sb.tile([P, 2], F32, name="msum", tag="msum", align_bytes=64)
+        msum = sb.tile([P, 2], F32, name="msum")
         m = sb.tile([P, 2], F32, name="m")
         nn = sb.tile([P, 2], F32, name="nn")
         ak = sb.tile([P, 2], F32, name="ak")
         f = [wide("ff1"), wide("ff2")]
         pc = [wide("pc1"), wide("pc2")]
+        pg = [wide("pg1"), wide("pg2")]
 
         def summed(dst, x, factor, y, total):
             vec.scalar_tensor_tensor(out=dst[:], in0=x[:], scalar=factor, in1=y[:], op0=ALU.mult, op1=ALU.mult, accum_out=total)
 
-        vec.reciprocal(out=rz[:], in_=z[:])
-        summed(pc[0], p[0], -1.0, c0, msum[:, 0:1])
-        vec.tensor_tensor(out=aa[:], in0=cf[:], in1=rz[:].unsqueeze(1).to_broadcast([P, 3, 2]), op=ALU.mult)
-        summed(pc[1], p[1], -1.0, c0, msum[:, 1:2])
-        vec.scalar_tensor_tensor(out=c1[:], in0=aa[:, 1, :], scalar=-1.0, in1=rz[:], op0=ALU.mult, op1=ALU.mult)
-        vec.scalar_tensor_tensor(out=m[:], in0=msum[:], scalar=-1.0, in1=rz[:], op0=ALU.mult, op1=ALU.mult)
-        pg = [wide("pg1", "msum"), wide("pg2")]
+        for h in range(2):
+            vec.reciprocal(out=rz[:, h : h + 1], in_=z[:, h : h + 1])
+            summed(pc[h], p[h], 1.0, c0, msum[:, h : h + 1])
+        for h in (1, 0):
+            act.activation(out=aa[:, h, :], in_=cf[:, h, :], func=ACT.Copy, scale=rz[:, h : h + 1])
+        for h in (1, 0):
+            act.activation(out=c1[:, h, :], in_=aa[:, h, 2:4], func=ACT.Copy, scale=rz[:, h : h + 1])
+        g4 = wide("g4")
+        act.copy(out=g4[:], in_=g_bank[:])
         for h in range(2):
             pool_eng.tensor_tensor(out=pg[h][:], in0=p[h][:], in1=g4[:], op=ALU.mult)
+            act.activation(out=m[:, h : h + 1], in_=msum[:, h : h + 1], func=ACT.Copy, scale=rz[:, h : h + 1])
         for h in (1, 0):
-            summed(wide("spent_t%d" % h), p[h], c1[:, h : h + 1], ts, tb[:, h : h + 1])
+            summed(wide("spent_t%d" % h), p[h], c1[:, h, 1:2], ts, tb[:, h : h + 1])
         f2a = wide("f2a")
-        act.activation(out=f2a[:], in_=ts_again[:], func=ACT.Identity, scale=aa[:, 2, 1:2], bias=tb[:, 1:2])
-        act.activation(out=f[0][:], in_=f_bank[:], func=ACT.Identity, scale=aa[:, 0, 0:1], bias=tb[:, 0:1])
+        for cs in halves:
+            act.activation(out=f2a[:, cs], in_=ts_again[:, cs], func=ACT.Identity, scale=aa[:, 1, 1:2], bias=tb[:, 1:2])
+            act.activation(out=f[0][:, cs], in_=f_bank[:, cs], func=ACT.Identity, scale=aa[:, 0, 0:1], bias=tb[:, 0:1])
         for h in range(2):
             col = slice(h, h + 1)
-            summed(wide("spent_n%d" % h), pc[h], c1[:, col], ts, nn[:, col])
+            summed(wide("spent_n%d" % h), pc[h], c1[:, h, 0:1], ts, nn[:, col])
             act.activation(out=ak[:, col], in_=tb[:, col], func=ACT.Identity, scale=m[:, col], bias=nn[:, col])
-        vec.scalar_tensor_tensor(out=f[1][:], in0=f_bank[:], scalar=aa[:, 0, 1:2], in1=f2a[:], op0=ALU.mult, op1=ALU.add)
+
+        base_banks = []
+        for c, (bank_tag, staged_tag) in enumerate((("a1", "spent_t0"), ("s_bank", "spent_n0"), ("ta", "spent_n1"))):
+            starts = range(EDGES[c], EDGES[c + 1], P)
+            width = EDGES[c + 1] - EDGES[c]
+            once = ps.tile([P, width], F32, name="base_once%d" % c, tag=bank_tag)
+            turn_into(once, [base_sb[:, t0 : t0 + P] for t0 in starts], True, True)
+            staged = sb.tile([P, width], F32, name="staged%d" % c, tag=staged_tag, align_bytes=64)
+            act.copy(out=staged[:], in_=once[:])
+            twice = ps.tile([P, width], F32, name="base_twice%d" % c, tag=bank_tag)
+            turn_into(twice, [staged[:, t0 - EDGES[c] : t0 - EDGES[c] + P] for t0 in starts], True, True)
+            base_banks.append(twice)
 
         for part in range(2):
             cs = slice(part * HALF, (part + 1) * HALF)
             picks = offsets[:, part * (HALF // 16) : (part + 1) * (HALF // 16)]
+            vec.scalar_tensor_tensor(out=f[1][:, cs], in0=f_bank[:, cs], scalar=aa[:, 1, 0:1], in1=f2a[:, cs], op0=ALU.mult, op1=ALU.add)
             b = [sb.tile([P, HALF], F32, name="b%d_%d" % (part, h)) for h in range(2)]
             o = [sb.tile([P, HALF], F32, name="o%d_%d" % (part, h)) for h in range(2)]
             for h in range(2):
@@ -272,8 +288,12 @@ def tile_attend_hvsaturating_twoheats_s_kernel(
             else:
                 vec.tensor_tensor(out=placed[:].indirect(picks), in0=o[0][:], in1=o[1][:], op=ALU.add)
 
+        rest = slice(EDGES[-1], T)
+        res_rest = sb.tile([P, T - EDGES[-1]], F32, name="res_rest")
+        pool_eng.tensor_tensor(out=res_rest[:], in0=placed[:, rest], in1=base_sb[:, rest], op=ALU.add)
         for c in range(len(EDGES) - 1):
             cs = slice(EDGES[c], EDGES[c + 1])
             res = sb.tile([P, EDGES[c + 1] - EDGES[c]], F32, name="res%d" % c)
-            vec.tensor_tensor(out=res[:], in0=placed[:, cs], in1=base_sb[:, cs], op=ALU.add)
+            vec.tensor_tensor(out=res[:], in0=placed[:, cs], in1=base_banks[c][:], op=ALU.add)
             nc.sync.dma_start(out=out[:, cs], in_=res[:])
+        act.dma_start(out=out[:, rest], in_=res_rest[:])

from contextlib import ExitStack

import concourse.mybir as mybir
from concourse.masks import make_identity

D, T, I, Q = 512, 2048, 512, 128
FLOPS = 3 * 2 * D * I * Q

F32 = mybir.dt.float32
BF16 = mybir.dt.bfloat16
I32 = mybir.dt.int32
U32 = mybir.dt.uint32
U16 = mybir.dt.uint16
U8 = mybir.dt.uint8
FP8X4 = mybir.dt.float8_e4m3fn_x4
ALU = mybir.AluOpType
ACT = mybir.ActivationFunctionType
P = 128
BLOCKS = I // P
HALF = I // 2
EDGES = (0, 512, 1024, 1408)


def tile_attend_hvsaturating_twoheats_s_kernel(
    tc, query, keys_words, keys_scales, ceil_t, halfp, sharp, share, gout, vals_words, vals_scales, dquery, base, offs, out
):
    nc = tc.nc
    vec, act, pe, pool_eng = nc.vector, nc.scalar, nc.tensor, nc.gpsimd
    with ExitStack() as ctx:
        sb = ctx.enter_context(tc.tile_pool(name="sb", bufs=1))
        ps = ctx.enter_context(tc.psum_pool(name="ps", bufs=1))

        def wide(name, tag=None):
            return sb.tile([P, I], F32, name=name, tag=tag or name, align_bytes=64)

        def load_scales(name, scales, zeroer):
            tile = sb.tile([P, T + 4], U8, name=name, tag=name, align_bytes=64)
            zeroer.memset(tile[:].bitcast(I32), 0)
            for quad in range(4):
                nc.sync.dma_start(out=tile[32 * quad : 32 * quad + 4, 0:T].bitcast(I32), in_=scales[0, 4 * quad : 4 * quad + 4, :].bitcast(I32))
            return tile

        def load_words(name, words, tag, queue):
            tile = sb.tile([P, T], U32, name=name, tag=tag, align_bytes=64)
            queue.dma_start(out=tile[:].bitcast(I32), in_=words[0].rearrange("p n t -> p (n t)").bitcast(I32))
            return tile

        def load_row(name, table, tag, zeroer, row):
            tile = sb.tile([P, T + 1], F32, name=name, tag=tag, align_bytes=64)
            zeroer.memset(tile[:], 0.0)
            nc.sync.dma_start(out=tile[row : row + 1, 0:T], in_=table[0:1, :])
            return tile

        def load_rows(name, rows, tag):
            raw = sb.tile([P, 4, Q], F32, name=name, tag=tag)
            nc.sync.dma_start(out=raw[:], in_=rows.rearrange("(p j) w -> p j w", j=4))
            return raw

        def scalar_cast(out, in_):
            act.activation(out=out, in_=in_, func=ACT.Copy)

        def quantise(name, raw, cast, tag):
            grouped = sb.tile([P, Q, 4], BF16, name=name + "_bf", tag=tag, align_bytes=64)
            cast(out=grouped[:], in_=raw[:].rearrange("p j w -> p w j"))
            codes = sb.tile([P, Q], U32, name=name + "_codes", align_bytes=64)
            scales = sb.tile([P, Q], U8, name=name + "_scales", align_bytes=64)
            vec.quantize_mx(out=codes[:].bitcast(FP8X4), scales=scales[:], in_=grouped[:].rearrange("p w j -> p (w j)"))
            return codes, scales

        def gather(name, window, dtype, tag, parts=1):
            picked = sb.tile([P, I], dtype, name=name, tag=tag, align_bytes=64)
            n = I // parts
            for j in range(parts):
                vec.tensor_copy(out=picked[:, j * n : (j + 1) * n], in_=window[:, 0:T].indirect(offsets[:, j * n // 16 : (j + 1) * n // 16]))
            return picked

        def product(name, rows, words, scales):
            bank = ps.tile([P, I], F32, name=name)
            pe.matmul_mx(out=bank[:], lhsT=rows[0][:].bitcast(FP8X4), lhsT_scale=rows[1][:], rhs=words[:].bitcast(FP8X4), rhs_scale=scales[:], start=True, stop=True)
            return bank

        def scores_by_slot(name, rows, words, scales, first, count):
            bank = ps.tile([P, count, Q], F32, name=name)
            for b in range(count):
                cs = slice((first + b) * P, (first + b + 1) * P)
                pe.matmul_mx(out=bank[:, b, :], lhsT=words[:, cs].bitcast(FP8X4), lhsT_scale=scales[:, cs], rhs=rows[0][:].bitcast(FP8X4), rhs_scale=rows[1][:], start=True, stop=True)
            return bank[:].rearrange("p b q -> p (b q)")

        def turn_into(bank, blocks, first, last):
            for b, block in enumerate(blocks):
                pe.matmul(out=bank[:, b * P : (b + 1) * P], lhsT=block, rhs=ident[:], is_transpose=True, start=first and b == 0, stop=last and b == len(blocks) - 1)

        def blocks_of(tile):
            return [tile[:, b * P : (b + 1) * P] for b in range(BLOCKS)]

        halves = [slice(0, HALF), slice(HALF, I)]
        offsets = sb.tile([P, I // 16], U16, name="offsets")
        nc.sync.dma_start(offsets[:], offs)
        q_raw = load_rows("q_raw", query, "rows_a")
        k_words = load_words("k_words", keys_words, "win_k", act)
        k_scales = load_scales("k_scales", keys_scales, vec)
        half_win = load_row("half_win", halfp, "win_h", pool_eng, 0)
        ceil_win = load_row("ceil_win", ceil_t, "win_c", vec, 1)
        ident = sb.tile([P, P], F32, name="ident")
        make_identity(nc, ident[:])
        v_scales = load_scales("v_scales", vals_scales, pool_eng)
        sharp_c = sb.tile([P, 1], F32, name="sharp_c")
        pool_eng.dma_start(out=sharp_c[:], in_=sharp)
        share_c = sb.tile([P, 1], F32, name="share_c")
        pool_eng.dma_start(out=share_c[:], in_=share)

        k_bytes = gather("k_bytes", k_scales, U8, "k_bytes")
        q_mx = quantise("q", q_raw, scalar_cast, "q_bf")
        placed = sb.tile([P, T], F32, name="placed", tag="q_bf", align_bytes=64)
        pool_eng.memset(placed[:], 0.0)
        dq_raw = load_rows("dq_raw", dquery, "rows_a")
        k_codes = gather("k_codes", k_words, U32, "k_codes", 2)
        a = [scores_by_slot("a%d" % j, q_mx, k_codes, k_bytes, 2 * j, 2) for j in range(2)]

        turned = ps.tile([P, I], F32, name="turned", tag="bank_g")
        for j, window in enumerate((half_win, ceil_win)):
            picked = wide("picked%d" % j)
            scalar_cast(out=picked[:], in_=window[:].indirect(offsets[:]))
            turn_into(turned, blocks_of(picked), j == 0, j == 1)
        v_words = load_words("v_words", vals_words, "k_scales", nc.sync)
        base_sb = sb.tile([P, T], F32, name="base_sb", tag="win_h", align_bytes=64)
        nc.sync.dma_start(out=base_sb[:], in_=base)

        nth = wide("nth", "win_c")
        for j, cs in enumerate(halves):
            act.activation(out=nth[:, cs], in_=a[j], func=ACT.Tanh, scale=-1.0)
        th_abs = wide("th_abs")
        vec.scalar_tensor_tensor(out=th_abs[:], in0=nth[:], scalar=-1.0, in1=nth[:], op0=ALU.mult, op1=ALU.max)
        lg = wide("lg")
        for cs in halves:
            act.activation(out=lg[:, cs], in_=th_abs[:, cs], func=ACT.Ln, scale=0.5, bias=0.5)
        rl = wide("rl")
        for j, cs in enumerate(halves):
            vec.tensor_scalar(out=rl[:, cs], in0=a[j], scalar1=0.0, scalar2=2.0, op0=ALU.max, op1=ALU.mult)

        hc = sb.tile([P, 2, BLOCKS], F32, name="hc")
        nk = sb.tile([P, BLOCKS], F32, name="nk")
        c3 = sb.tile([P, BLOCKS], F32, name="c3")
        vec.tensor_copy(out=hc[:], in_=turned[:].rearrange("p (b q) -> p q b", b=BLOCKS)[:, 0:2, :])
        hh, cc = hc[:, 0, :], hc[:, 1, :]
        vec.scalar_tensor_tensor(out=nk[:], in0=cc, scalar=-1.0, in1=hh, op0=ALU.mult, op1=ALU.mult)
        vec.scalar_tensor_tensor(out=c3[:], in0=nk[:], scalar=0.5, in1=hh, op0=ALU.mult, op1=ALU.add)

        fh = wide("fh")
        for cs in halves:
            vec.tensor_tensor(out=fh[:, cs], in0=rl[:, cs], in1=lg[:, cs], op=ALU.subtract)
        y2 = wide("y2")
        for b in range(BLOCKS):
            act.activation(out=blocks_of(y2)[b], in_=blocks_of(fh)[b], func=ACT.Square, bias=hh[:, b : b + 1])
        ly = wide("ly")
        act.activation(out=ly[:], in_=y2[:], func=ACT.Ln)
        qq = wide("qq")
        for cs in halves:
            act.activation(out=qq[:, cs], in_=ly[:, cs], func=ACT.Exp, scale=-1.0)

        s_bank = ps.tile([P, I], F32, name="s_bank", tag="s_bank")
        turn_into(s_bank, [cc[:, b : b + 1].to_broadcast([P, P]) for b in range(BLOCKS)], True, False)
        nyk = wide("nyk")
        for b in range(BLOCKS):
            pool_eng.tensor_scalar(out=blocks_of(nyk)[b], in0=blocks_of(fh)[b], scalar1=hh[:, b : b + 1], scalar2=nk[:, b : b + 1], op0=ALU.add, op1=ALU.mult)
        fc = wide("fc", "y2")
        for b in range(BLOCKS):
            act.activation(out=blocks_of(fc)[b], in_=blocks_of(fh)[b], func=ACT.Identity, bias=c3[:, b : b + 1])
        dq_mx = quantise("dq", dq_raw, vec.tensor_copy, "dq_bf")
        ta = scores_by_slot("ta", dq_mx, k_codes, k_bytes, 0, BLOCKS)
        pb1 = wide("pb1")
        vec.scalar_tensor_tensor(out=pb1[:], in0=nth[:], scalar=1.0, in1=ta, op0=ALU.add, op1=ALU.mult)
        f_bank = ps.tile([P, I], F32, name="f_bank")
        turn_into(f_bank, blocks_of(pb1), True, False)
        go_raw = load_rows("go_raw", gout, "rows_a")
        go_mx = quantise("go", go_raw, scalar_cast, "ly")
        v_bytes = gather("v_bytes", v_scales, U8, "lg")
        v_codes = gather("v_codes", v_words, U32, "rl")
        c0 = product("c0", go_mx, v_codes, v_bytes)

        cf = sb.tile([P, 2, 4], F32, name="cf")
        shm1 = sb.tile([P, 1], F32, name="shm1")
        beta = sb.tile([P, 1], F32, name="beta")
        pool_eng.tensor_scalar(out=shm1[:], in0=sharp_c[:], scalar1=-1.0, scalar2=1.0, op0=ALU.add, op1=ALU.mult)
        pool_eng.tensor_scalar(out=beta[:], in0=share_c[:], scalar1=-1.0, scalar2=sharp_c[:], op0=ALU.add, op1=ALU.mult)
        for j, factor in enumerate((512.0, 0.0, 256.0, -256.0)):
            pool_eng.tensor_scalar(out=cf[:, 0, j : j + 1], in0=share_c[:], scalar1=factor, scalar2=1.0, op0=ALU.mult, op1=ALU.mult)
        for j, (factor, other) in enumerate(((512.0, 1.0), (256.0, shm1[:]), (256.0, sharp_c[:]), (-256.0, sharp_c[:]))):
            pool_eng.tensor_scalar(out=cf[:, 1, j : j + 1], in0=beta[:], scalar1=factor, scalar2=other, op0=ALU.mult, op1=ALU.mult)

        nv = wide("nv")
        for cs in halves:
            vec.tensor_tensor(out=nv[:, cs], in0=nyk[:, cs], in1=qq[:, cs], op=ALU.mult)
        turn_into(s_bank, blocks_of(nv), False, True)
        low = sb.tile([P, 2], F32, name="low")
        ns = [wide("ns1"), wide("ns2")]
        vec.tensor_scalar(out=ns[0][:], in0=s_bank[:], scalar1=-1.0, scalar2=None, op0=ALU.mult, op1=ALU.min, accum_out=low[:, 0:1])
        vec.tensor_scalar(out=ns[1][:], in0=ns[0][:], scalar1=sharp_c[:], scalar2=None, op0=ALU.mult, op1=ALU.min, accum_out=low[:, 1:2])
        z = sb.tile([P, 2], F32, name="z")
        p = [wide("p1"), wide("p2")]
        for h in range(2):
            act.activation(out=p[h][:], in_=ns[h][:], func=ACT.Exp, scale=-1.0, bias=low[:, h : h + 1], accum_out=z[:, h : h + 1])

        gq = wide("gq")
        vec.scalar_tensor_tensor(out=gq[:], in0=nth[:], scalar=-1.0, in1=qq[:], op0=ALU.add, op1=ALU.mult)
        tq = wide("tq")
        vec.scalar_tensor_tensor(out=tq[:], in0=ta, scalar=2.0, in1=gq[:], op0=ALU.mult, op1=ALU.mult)
        tst = wide("tst")
        for b in range(BLOCKS):
            act.activation(out=blocks_of(tst)[b], in_=blocks_of(tq)[b], func=ACT.Copy, scale=nk[:, b : b + 1])
        ts = ps.tile([P, I], F32, name="ts")
        turn_into(ts, blocks_of(tst), True, True)
        ts_again = ps.tile([P, I], F32, name="ts_again", tag="a0")
        turn_into(ts_again, blocks_of(tst), True, True)
        dqq = wide("dqq")
        pool_eng.tensor_tensor(out=dqq[:], in0=fc[:], in1=tq[:], op=ALU.mult)
        turn_into(f_bank, blocks_of(dqq), False, True)
        g4t = wide("g4t")
        for b in range(BLOCKS):
            act.activation(out=blocks_of(g4t)[b], in_=blocks_of(gq)[b], func=ACT.Copy, scale=nk[:, b : b + 1])
        g_bank = ps.tile([P, I], F32, name="g_bank", tag="bank_g")
        turn_into(g_bank, blocks_of(g4t), True, True)

        rz = sb.tile([P, 2], F32, name="rz")
        aa = sb.tile([P, 2, 4], F32, name="aa")
        c1 = sb.tile([P, 2, 2], F32, name="c1")
        tb = sb.tile([P, 2], F32, name="tb")
        msum = sb.tile([P, 2], F32, name="msum")
        m = sb.tile([P, 2], F32, name="m")
        nn = sb.tile([P, 2], F32, name="nn")
        ak = sb.tile([P, 2], F32, name="ak")
        f = [wide("ff1"), wide("ff2")]
        pc = [wide("pc1"), wide("pc2")]
        pg = [wide("pg1"), wide("pg2")]

        def summed(dst, x, factor, y, total):
            vec.scalar_tensor_tensor(out=dst[:], in0=x[:], scalar=factor, in1=y[:], op0=ALU.mult, op1=ALU.mult, accum_out=total)

        for h in range(2):
            vec.reciprocal(out=rz[:, h : h + 1], in_=z[:, h : h + 1])
            summed(pc[h], p[h], 1.0, c0, msum[:, h : h + 1])
        for h in (1, 0):
            act.activation(out=aa[:, h, :], in_=cf[:, h, :], func=ACT.Copy, scale=rz[:, h : h + 1])
        for h in (1, 0):
            act.activation(out=c1[:, h, :], in_=aa[:, h, 2:4], func=ACT.Copy, scale=rz[:, h : h + 1])
        g4 = wide("g4")
        act.copy(out=g4[:], in_=g_bank[:])
        for h in range(2):
            pool_eng.tensor_tensor(out=pg[h][:], in0=p[h][:], in1=g4[:], op=ALU.mult)
            act.activation(out=m[:, h : h + 1], in_=msum[:, h : h + 1], func=ACT.Copy, scale=rz[:, h : h + 1])
        for h in (1, 0):
            summed(wide("spent_t%d" % h), p[h], c1[:, h, 1:2], ts, tb[:, h : h + 1])
        f2a = wide("f2a")
        for cs in halves:
            act.activation(out=f2a[:, cs], in_=ts_again[:, cs], func=ACT.Identity, scale=aa[:, 1, 1:2], bias=tb[:, 1:2])
            act.activation(out=f[0][:, cs], in_=f_bank[:, cs], func=ACT.Identity, scale=aa[:, 0, 0:1], bias=tb[:, 0:1])
        for h in range(2):
            col = slice(h, h + 1)
            summed(wide("spent_n%d" % h), pc[h], c1[:, h, 0:1], ts, nn[:, col])
            act.activation(out=ak[:, col], in_=tb[:, col], func=ACT.Identity, scale=m[:, col], bias=nn[:, col])

        base_banks = []
        for c, (bank_tag, staged_tag) in enumerate((("a1", "spent_t0"), ("s_bank", "spent_n0"), ("ta", "spent_n1"))):
            starts = range(EDGES[c], EDGES[c + 1], P)
            width = EDGES[c + 1] - EDGES[c]
            once = ps.tile([P, width], F32, name="base_once%d" % c, tag=bank_tag)
            turn_into(once, [base_sb[:, t0 : t0 + P] for t0 in starts], True, True)
            staged = sb.tile([P, width], F32, name="staged%d" % c, tag=staged_tag, align_bytes=64)
            act.copy(out=staged[:], in_=once[:])
            twice = ps.tile([P, width], F32, name="base_twice%d" % c, tag=bank_tag)
            turn_into(twice, [staged[:, t0 - EDGES[c] : t0 - EDGES[c] + P] for t0 in starts], True, True)
            base_banks.append(twice)

        for part in range(2):
            cs = slice(part * HALF, (part + 1) * HALF)
            picks = offsets[:, part * (HALF // 16) : (part + 1) * (HALF // 16)]
            vec.scalar_tensor_tensor(out=f[1][:, cs], in0=f_bank[:, cs], scalar=aa[:, 1, 0:1], in1=f2a[:, cs], op0=ALU.mult, op1=ALU.add)
            b = [sb.tile([P, HALF], F32, name="b%d_%d" % (part, h)) for h in range(2)]
            o = [sb.tile([P, HALF], F32, name="o%d_%d" % (part, h)) for h in range(2)]
            for h in range(2):
                vec.scalar_tensor_tensor(out=b[h][:], in0=c0[:, cs], scalar=m[:, h : h + 1], in1=f[h][:, cs], op0=ALU.subtract, op1=ALU.mult)
            for h in range(2):
                vec.scalar_tensor_tensor(out=o[h][:], in0=b[h][:], scalar=ak[:, h : h + 1], in1=pg[h][:, cs], op0=ALU.subtract, op1=ALU.mult)
            if part == 0:
                gs = sb.tile([P, HALF], F32, name="gs")
                vec.tensor_tensor(out=gs[:], in0=o[0][:], in1=o[1][:], op=ALU.add)
                act.activation(out=placed[:].indirect(picks), in_=gs[:], func=ACT.Copy)
            else:
                vec.tensor_tensor(out=placed[:].indirect(picks), in0=o[0][:], in1=o[1][:], op=ALU.add)

        rest = slice(EDGES[-1], T)
        res_rest = sb.tile([P, T - EDGES[-1]], F32, name="res_rest")
        pool_eng.tensor_tensor(out=res_rest[:], in0=placed[:, rest], in1=base_sb[:, rest], op=ALU.add)
        for c in range(len(EDGES) - 1):
            cs = slice(EDGES[c], EDGES[c + 1])
            res = sb.tile([P, EDGES[c + 1] - EDGES[c]], F32, name="res%d" % c)
            vec.tensor_tensor(out=res[:], in0=placed[:, cs], in1=base_banks[c][:], op=ALU.add)
            nc.sync.dma_start(out=out[:, cs], in_=res[:])
        act.dma_start(out=out[:, rest], in_=res_rest[:])
